import numpy as np
import ml_dtypes


def mxq(x, axis, fmt="e4m3"):
    dtype, down = {"e4m3": (ml_dtypes.float8_e4m3fn, 7), "e5m2": (ml_dtypes.float8_e5m2, 14)}[fmt]
    v = np.moveaxis(np.asarray(x, np.float32).astype(ml_dtypes.bfloat16).astype(np.float64), axis, -1)
    blocks = v.reshape(v.shape[:-1] + (-1, 32))
    amax = np.abs(blocks).max(-1, keepdims=True)
    byte = np.maximum(np.where(amax > 0, np.frexp(amax)[1] - 1 + 127, 0) - down, 1)
    scale = np.exp2(byte - 127.0)
    codes = (blocks / scale).astype(np.float32).astype(dtype).astype(np.float64)
    return np.moveaxis((codes * scale).reshape(v.shape), -1, axis)


WIDE = False


def mx_kscale(k):
    if not WIDE:
        return np.ones(k)
    levels = np.array([10, -10, 5, -5, 0])
    if k % 512:
        return np.exp2(np.random.permutation(np.resize(levels, k // 32))).repeat(32)
    a = np.empty((k // 512, 16))
    for p in range(k // 512):
        a[p, :8] = np.random.permutation(np.resize(levels, 8))
        for g in range(8):
            far = levels[np.abs(levels - a[p, g]) >= 10]
            a[p, g + 8] = far[np.random.randint(len(far))]
    return np.exp2(a.ravel()).repeat(32)


def f64(x):
    return np.asarray(x).astype(np.float64)


def striped(idx):
    return np.tile(np.asarray(idx).reshape(-1, 16).T, (8, 1)).astype(np.uint16)


def unstriped(offs):
    return offs[:16].T.reshape(-1).astype(np.int64)


E2M1 = np.array([0.0, 0.5, 1.0, 1.5, 2.0, 3.0, 4.0, 6.0, -0.0, -0.5, -1.0, -1.5, -2.0, -3.0, -4.0, -6.0])


def pack_weight(w, fmt):
    k, n = w.shape
    w = f64(np.asarray(w, np.float32).astype(ml_dtypes.bfloat16)).reshape(k // 32, 32, n)
    amax = np.abs(w).max(1)
    if fmt == "e4m3":
        byte = np.frexp(amax)[1] - 1 + 127 - 7
    else:
        mant, ex = np.frexp(amax / 6.0)
        byte = np.where(mant > 0.5, ex, ex - 1) + 127
    byte = np.clip(np.where(amax > 0, byte, 1), 1, 254)
    scaled = (w * np.exp2(127.0 - byte)[:, None, :]).reshape(k, n).astype(np.float32)
    by_word = np.ascontiguousarray(scaled.reshape(k // 512, 128, 4, n).transpose(0, 1, 3, 2))
    if fmt == "e4m3":
        words = by_word.astype(ml_dtypes.float8_e4m3fn).view(np.uint8)
    else:
        c = by_word.astype(ml_dtypes.float4_e2m1fn).view(np.uint8) & 0xF
        words = (c[..., 0::2] | (c[..., 1::2] << 4)).reshape(k // 512, 128, 2 * n)
    return np.ascontiguousarray(words), np.ascontiguousarray(byte.astype(np.uint8).reshape(k // 512, 16, n))


def unpack_weight(words, scales, fmt):
    g, _, n = scales.shape
    words = np.ascontiguousarray(words).reshape(g, 128, n, -1)
    if fmt == "e4m3":
        vals = words.view(ml_dtypes.float8_e4m3fn).astype(np.float64)
    else:
        nib = np.empty((g, 128, n, 4), np.uint8)
        nib[..., 0::2] = words & 0xF
        nib[..., 1::2] = words >> 4
        vals = E2M1[nib]
    vals = vals * np.repeat(np.exp2(scales.astype(np.float64) - 127.0), 8, axis=1)[..., None]
    return vals.transpose(0, 1, 3, 2).reshape(g * 512, n)


B, N, T, D, NQ = 1, 512, 2048, 512, 512


def setup_inputs():
    n = np.random.standard_normal
    idx = np.random.permutation(T)[:B * N]
    s = mx_kscale(D)[:, None]
    kp = pack_weight(n((D, T)) / s, "e4m3")
    return {
        "qT": (n((B, D, NQ)) * s * (1.00 / np.sqrt(D))).astype(np.float32),
        "k_words": kp[0],
        "k_scales": kp[1],
        "kn": np.tile(np.random.uniform(1.0, 4.0, 2048), (128, 1)).astype(np.float32),
        "qn": (np.random.uniform(1.0, 4.0, (B, 1, NQ))).astype(np.float32),
        "offs": striped(idx),
    }


def reference(qT, k_words, k_scales, kn, qn, offs):
    idx = unstriped(offs)
    pick = lambda x, which: x[:, which].reshape(x.shape[0], B, -1).transpose(1, 0, 2)
    k = unpack_weight(k_words, k_scales, "e4m3")
    kg = pick(k, idx)
    qq = mxq(f64(qT), 1, "e4m3")
    a = kg.transpose(0, 2, 1) @ qq
    y = pick(f64(kn), idx)[:, :1, :].transpose(0, 2, 1) + f64(qn) - 2.0 * a
    return y

@@ -1,0 +1,115 @@
+from contextlib import ExitStack
+
+import concourse.mybir as mybir
+from concourse.masks import make_identity
+
+T, N, D, NQ = 2048, 512, 512, 512
+FLOPS = 2 * N * D * NQ
+
+F32 = mybir.dt.float32
+BF16 = mybir.dt.bfloat16
+I32 = mybir.dt.int32
+U32 = mybir.dt.uint32
+U16 = mybir.dt.uint16
+U8 = mybir.dt.uint8
+FP8X4 = mybir.dt.float8_e4m3fn_x4
+ADD = mybir.AluOpType.add
+MULT = mybir.AluOpType.mult
+COPY = mybir.ActivationFunctionType.Copy
+
+P = 128
+PACK = 4
+KN_ROW = P - 1
+SCALAR_COLS = 192
+
+
+def tile_attend_tok_dist_topk_kernel(tc, qT, k_words, k_scales, kn, qn, offs, out):
+    nc = tc.nc
+    with ExitStack() as ctx:
+        held = ctx.enter_context(tc.tile_pool(name="held", bufs=1))
+        psum = ctx.enter_context(tc.psum_pool(name="psum", bufs=1))
+
+        offsets = held.tile([P, N // 16], U16, name="offsets")
+        nc.sync.dma_start(offsets[:], offs)
+
+        scale_pool = held.tile([P, T], U8, name="scale_pool", align_bytes=64)
+        kn_pool = held.tile([P, T], F32, name="kn_pool", align_bytes=64)
+        word_pool = held.tile([P, T], U32, name="word_pool", align_bytes=64)
+        q_raw = held.tile([P, PACK, NQ], F32, name="q_raw", align_bytes=64)
+        qn_cols = held.tile([P, PACK], F32, name="qn_cols", align_bytes=64)
+
+        nc.vector.memset(scale_pool[:].bitcast(I32), 0)
+        nc.vector.memset(kn_pool[0:KN_ROW, :], 0.0)
+
+        nc.sync.dma_start(q_raw[:], qT[0].rearrange("(p j) w -> p j w", j=PACK))
+        nc.sync.dma_start(word_pool[:].bitcast(I32), k_words[0].rearrange("p t r -> p (t r)").bitcast(I32))
+
+        nc.scalar.dma_start(kn_pool[KN_ROW:P, :], kn[0:1, :])
+        for quad in range(4):
+            nc.scalar.dma_start(
+                scale_pool[32 * quad : 32 * quad + 4, :].bitcast(I32),
+                k_scales[0, 4 * quad : 4 * quad + 4, :].bitcast(I32),
+            )
+        nc.scalar.dma_start(qn_cols[:], qn[0, 0].rearrange("(p j) -> p j", j=PACK))
+
+        ident = held.tile([P, P], F32, name="ident", align_bytes=64)
+        make_identity(nc, ident[:])
+
+        kn_listed = held.tile([P, N], F32, name="kn_listed", align_bytes=64)
+        nc.vector.tensor_copy(kn_listed[:], kn_pool[:].indirect(offsets[:]))
+        k_scale = held.tile([P, N], U8, name="k_scale", align_bytes=64)
+        nc.vector.tensor_copy(k_scale[:], scale_pool[:].indirect(offsets[:]))
+
+        qn_ps = psum.tile([P, PACK, P], F32, name="qn_ps")
+        for j in range(PACK):
+            nc.tensor.transpose(qn_ps[:, j, :], qn_cols[:, j : j + 1].to_broadcast([P, P]), ident[:])
+        qn_rows = held.tile([P, NQ], F32, name="qn_rows", align_bytes=64)
+        nc.scalar.copy(qn_rows[:].rearrange("p (c j) -> p c j", j=PACK), qn_ps[:].rearrange("p j c -> p c j"))
+
+        kn_ps = psum.tile([P, N // P, P], F32, name="kn_ps")
+        for m in range(N // P):
+            nc.tensor.transpose(kn_ps[:, m, :], kn_listed[:, m * P : (m + 1) * P], ident[:])
+        kn_cols = held.tile([P, N // P], F32, name="kn_cols", align_bytes=64)
+        nc.scalar.copy(kn_cols[:], kn_ps[:, :, KN_ROW])
+
+        q_bf = held.tile([P, NQ, PACK], BF16, name="q_bf", align_bytes=64)
+
+        def views(c0, c1):
+            dst = q_bf[:, c0:c1, :].rearrange("p (c i) t -> p c t i", i=4)
+            src = q_raw[:, :, c0:c1].rearrange("p t (c i) -> p c t i", i=4)
+            return dst, src
+
+        dst, src = views(0, SCALAR_COLS)
+        nc.scalar.activation(dst, src, COPY, scale=-2.0)
+        dst, src = views(SCALAR_COLS, NQ)
+        nc.vector.tensor_scalar(dst, src, -2.0, None, MULT)
+
+        q_codes = held.tile([P, NQ], U32, name="q_codes", align_bytes=64)
+        q_scale = held.tile([P, NQ], U8, name="q_scale", align_bytes=64)
+        nc.vector.quantize_mx(
+            out=q_codes[:].bitcast(FP8X4), scales=q_scale[:], in_=q_bf[:].rearrange("p c t -> p (c t)")
+        )
+
+        k_codes = held.tile([P, N], U32, name="k_codes", align_bytes=64)
+        half = N // 2
+        for h in range(2):
+            nc.vector.tensor_copy(
+                k_codes[:, h * half : (h + 1) * half],
+                word_pool[:].indirect(offsets[:, h * half // 16 : (h + 1) * half // 16]),
+            )
+
+        for m in range(N // P):
+            slots = slice(m * P, (m + 1) * P)
+            acc = psum.tile([P, NQ], F32, name="acc%d" % m)
+            nc.tensor.matmul_mx(
+                out=acc[:],
+                lhsT=k_codes[:, slots].bitcast(FP8X4),
+                lhsT_scale=k_scale[:, slots],
+                rhs=q_codes[:].bitcast(FP8X4),
+                rhs_scale=q_scale[:],
+                start=True,
+                stop=True,
+            )
+            res = held.tile([P, NQ], F32, name="res%d" % m, align_bytes=64)
+            nc.vector.scalar_tensor_tensor(res[:], acc[:], kn_cols[:, m : m + 1], qn_rows[:], ADD, ADD)
+            nc.sync.dma_start(out[0, slots, :], res[:])

@@ -20,7 +20,8 @@ COPY = mybir.ActivationFunctionType.Copy
 P = 128
 PACK = 4
 KN_ROW = P - 1
-SCALAR_COLS = 192
+HALF = NQ // 2
+SCALAR_COLS = (112, 160)
 
 
 def tile_attend_tok_dist_topk_kernel(tc, qT, k_words, k_scales, kn, qn, offs, out):
@@ -35,81 +36,100 @@ def tile_attend_tok_dist_topk_kernel(tc, qT, k_words, k_scales, kn, qn, offs, ou
         scale_pool = held.tile([P, T], U8, name="scale_pool", align_bytes=64)
         kn_pool = held.tile([P, T], F32, name="kn_pool", align_bytes=64)
         word_pool = held.tile([P, T], U32, name="word_pool", align_bytes=64)
-        q_raw = held.tile([P, PACK, NQ], F32, name="q_raw", align_bytes=64)
+        q_raw = [held.tile([P, PACK, HALF], F32, name="q_raw%d" % h, align_bytes=64) for h in range(2)]
         qn_cols = held.tile([P, PACK], F32, name="qn_cols", align_bytes=64)
 
-        nc.vector.memset(scale_pool[:].bitcast(I32), 0)
+        nc.gpsimd.memset(scale_pool[:].bitcast(I32), 0)
         nc.vector.memset(kn_pool[0:KN_ROW, :], 0.0)
 
-        nc.sync.dma_start(q_raw[:], qT[0].rearrange("(p j) w -> p j w", j=PACK))
-        nc.sync.dma_start(word_pool[:].bitcast(I32), k_words[0].rearrange("p t r -> p (t r)").bitcast(I32))
+        q_rows = qT[0].rearrange("(p j) w -> p j w", j=PACK)
+        scale_rows = k_scales[0].rearrange("(q r) t -> r q t", r=4)
 
-        nc.scalar.dma_start(kn_pool[KN_ROW:P, :], kn[0:1, :])
-        for quad in range(4):
-            nc.scalar.dma_start(
-                scale_pool[32 * quad : 32 * quad + 4, :].bitcast(I32),
-                k_scales[0, 4 * quad : 4 * quad + 4, :].bitcast(I32),
-            )
+        def load_scales(eng):
+            for r in range(4):
+                eng.dma_start(scale_pool[r:P:32, :].bitcast(I32), scale_rows[r].bitcast(I32))
+
         nc.scalar.dma_start(qn_cols[:], qn[0, 0].rearrange("(p j) -> p j", j=PACK))
+        nc.sync.dma_start(kn_pool[KN_ROW:P, :], kn[0:1, :])
+        nc.sync.dma_start(q_raw[0][:], q_rows[:, :, 0:HALF])
+        load_scales(nc.sync)
+        nc.sync.dma_start(word_pool[:].bitcast(I32), k_words[0].rearrange("p t r -> p (t r)").bitcast(I32))
+        nc.sync.dma_start(q_raw[1][:], q_rows[:, :, HALF:NQ])
 
         ident = held.tile([P, P], F32, name="ident", align_bytes=64)
         make_identity(nc, ident[:])
 
         kn_listed = held.tile([P, N], F32, name="kn_listed", align_bytes=64)
         nc.vector.tensor_copy(kn_listed[:], kn_pool[:].indirect(offsets[:]))
-        k_scale = held.tile([P, N], U8, name="k_scale", align_bytes=64)
-        nc.vector.tensor_copy(k_scale[:], scale_pool[:].indirect(offsets[:]))
 
-        qn_ps = psum.tile([P, PACK, P], F32, name="qn_ps")
+        qn_ps = psum.tile([P, PACK, P], F32, name="qn_ps", tag="bank6")
         for j in range(PACK):
             nc.tensor.transpose(qn_ps[:, j, :], qn_cols[:, j : j + 1].to_broadcast([P, P]), ident[:])
-        qn_rows = held.tile([P, NQ], F32, name="qn_rows", align_bytes=64)
-        nc.scalar.copy(qn_rows[:].rearrange("p (c j) -> p c j", j=PACK), qn_ps[:].rearrange("p j c -> p c j"))
-
-        kn_ps = psum.tile([P, N // P, P], F32, name="kn_ps")
+        kn_ps = psum.tile([P, N // P, P], F32, name="kn_ps", tag="bank7")
         for m in range(N // P):
             nc.tensor.transpose(kn_ps[:, m, :], kn_listed[:, m * P : (m + 1) * P], ident[:])
+
+        q_bf = [held.tile([P, HALF, PACK], BF16, name="q_bf%d" % h, align_bytes=64) for h in range(2)]
+        q_codes = [held.tile([P, HALF], U32, name="q_codes%d" % h, align_bytes=64) for h in range(2)]
+        q_scale = [held.tile([P, HALF], U8, name="q_scale%d" % h, align_bytes=64) for h in range(2)]
+
+        def views(h, c0, c1):
+            dst = q_bf[h][:, c0:c1, :].rearrange("p (c i) t -> p c t i", i=4)
+            src = q_raw[h][:, :, c0:c1].rearrange("p t (c i) -> p c t i", i=4)
+            return dst, src
+
+        def quantize(h):
+            nc.vector.quantize_mx(
+                out=q_codes[h][:].bitcast(FP8X4), scales=q_scale[h][:], in_=q_bf[h][:].rearrange("p c t -> p (c t)")
+            )
+
+        dst, src = views(0, 0, SCALAR_COLS[0])
+        nc.scalar.activation(dst, src, COPY, scale=-2.0)
+        dst, src = views(0, SCALAR_COLS[0], HALF)
+        nc.vector.tensor_scalar(dst, src, -2.0, None, MULT)
+        quantize(0)
+
+        qn_rows = held.tile([P, NQ], F32, name="qn_rows", align_bytes=64)
+        nc.scalar.copy(qn_rows[:].rearrange("p (c j) -> p c j", j=PACK), qn_ps[:].rearrange("p j c -> p c j"))
         kn_cols = held.tile([P, N // P], F32, name="kn_cols", align_bytes=64)
         nc.scalar.copy(kn_cols[:], kn_ps[:, :, KN_ROW])
 
-        q_bf = held.tile([P, NQ, PACK], BF16, name="q_bf", align_bytes=64)
-
-        def views(c0, c1):
-            dst = q_bf[:, c0:c1, :].rearrange("p (c i) t -> p c t i", i=4)
-            src = q_raw[:, :, c0:c1].rearrange("p t (c i) -> p c t i", i=4)
-            return dst, src
-
-        dst, src = views(0, SCALAR_COLS)
-        nc.scalar.activation(dst, src, COPY, scale=-2.0)
-        dst, src = views(SCALAR_COLS, NQ)
-        nc.vector.tensor_scalar(dst, src, -2.0, None, MULT)
-
-        q_codes = held.tile([P, NQ], U32, name="q_codes", align_bytes=64)
-        q_scale = held.tile([P, NQ], U8, name="q_scale", align_bytes=64)
-        nc.vector.quantize_mx(
-            out=q_codes[:].bitcast(FP8X4), scales=q_scale[:], in_=q_bf[:].rearrange("p c t -> p (c t)")
-        )
+        k_scale = held.tile([P, N], U8, name="k_scale", align_bytes=64)
+        nc.vector.tensor_copy(k_scale[:], scale_pool[:].indirect(offsets[:]))
 
         k_codes = held.tile([P, N], U32, name="k_codes", align_bytes=64)
-        half = N // 2
-        for h in range(2):
+        for g in range(2):
             nc.vector.tensor_copy(
-                k_codes[:, h * half : (h + 1) * half],
-                word_pool[:].indirect(offsets[:, h * half // 16 : (h + 1) * half // 16]),
+                k_codes[:, g * N // 2 : (g + 1) * N // 2],
+                word_pool[:].indirect(offsets[:, g * N // 32 : (g + 1) * N // 32]),
             )
 
-        for m in range(N // P):
-            slots = slice(m * P, (m + 1) * P)
-            acc = psum.tile([P, NQ], F32, name="acc%d" % m)
-            nc.tensor.matmul_mx(
-                out=acc[:],
-                lhsT=k_codes[:, slots].bitcast(FP8X4),
-                lhsT_scale=k_scale[:, slots],
-                rhs=q_codes[:].bitcast(FP8X4),
-                rhs_scale=q_scale[:],
-                start=True,
-                stop=True,
-            )
-            res = held.tile([P, NQ], F32, name="res%d" % m, align_bytes=64)
-            nc.vector.scalar_tensor_tensor(res[:], acc[:], kn_cols[:, m : m + 1], qn_rows[:], ADD, ADD)
-            nc.sync.dma_start(out[0, slots, :], res[:])
+        dst, src = views(1, 0, SCALAR_COLS[1])
+        nc.scalar.activation(dst, src, COPY, scale=-2.0)
+        nc.gpsimd.tensor_scalar(
+            q_bf[1][:, SCALAR_COLS[1] :, :],
+            q_raw[1][:, :, SCALAR_COLS[1] :].rearrange("p t c -> p c t"),
+            -2.0,
+            0.0,
+            MULT,
+            ADD,
+        )
+        quantize(1)
+
+        for h in range(2):
+            cols = slice(h * HALF, (h + 1) * HALF)
+            for m in range(N // P):
+                slots = slice(m * P, (m + 1) * P)
+                acc = psum.tile([P, HALF], F32, name="acc%d_%d" % (h, m), tag="bank%d" % (4 * h + m))
+                nc.tensor.matmul_mx(
+                    out=acc[:],
+                    lhsT=k_codes[:, slots].bitcast(FP8X4),
+                    lhsT_scale=k_scale[:, slots],
+                    rhs=q_codes[h][:].bitcast(FP8X4),
+                    rhs_scale=q_scale[h][:],
+                    start=True,
+                    stop=True,
+                )
+                res = held.tile([P, HALF], F32, name="res%d_%d" % (h, m), align_bytes=64)
+                nc.vector.scalar_tensor_tensor(res[:], acc[:], kn_cols[:, m : m + 1], qn_rows[:, cols], ADD, ADD)
+                nc.sync.dma_start(out[0, slots, cols], res[:])

@@ -20,8 +20,8 @@ COPY = mybir.ActivationFunctionType.Copy
 P = 128
 PACK = 4
 KN_ROW = P - 1
-HALF = NQ // 2
-SCALAR_COLS = (112, 160)
+EARLY = 512
+SCALAR_COLS = 352
 
 
 def tile_attend_tok_dist_topk_kernel(tc, qT, k_words, k_scales, kn, qn, offs, out):
@@ -36,7 +36,7 @@ def tile_attend_tok_dist_topk_kernel(tc, qT, k_words, k_scales, kn, qn, offs, ou
         scale_pool = held.tile([P, T], U8, name="scale_pool", align_bytes=64)
         kn_pool = held.tile([P, T], F32, name="kn_pool", align_bytes=64)
         word_pool = held.tile([P, T], U32, name="word_pool", align_bytes=64)
-        q_raw = [held.tile([P, PACK, HALF], F32, name="q_raw%d" % h, align_bytes=64) for h in range(2)]
+        q_early = held.tile([P, PACK, EARLY], F32, name="q_early", align_bytes=64)
         qn_cols = held.tile([P, PACK], F32, name="qn_cols", align_bytes=64)
 
         nc.gpsimd.memset(scale_pool[:].bitcast(I32), 0)
@@ -45,22 +45,23 @@ def tile_attend_tok_dist_topk_kernel(tc, qT, k_words, k_scales, kn, qn, offs, ou
         q_rows = qT[0].rearrange("(p j) w -> p j w", j=PACK)
         scale_rows = k_scales[0].rearrange("(q r) t -> r q t", r=4)
 
-        def load_scales(eng):
-            for r in range(4):
+        def load_scales(eng, rows):
+            for r in rows:
                 eng.dma_start(scale_pool[r:P:32, :].bitcast(I32), scale_rows[r].bitcast(I32))
 
+        nc.scalar.dma_start(kn_pool[KN_ROW:P, :], kn[0:1, :])
         nc.scalar.dma_start(qn_cols[:], qn[0, 0].rearrange("(p j) -> p j", j=PACK))
-        nc.sync.dma_start(kn_pool[KN_ROW:P, :], kn[0:1, :])
-        nc.sync.dma_start(q_raw[0][:], q_rows[:, :, 0:HALF])
-        load_scales(nc.sync)
+        nc.sync.dma_start(q_early[:], q_rows[:, :, 0:EARLY])
+        load_scales(nc.sync, (0, 1, 2, 3))
         nc.sync.dma_start(word_pool[:].bitcast(I32), k_words[0].rearrange("p t r -> p (t r)").bitcast(I32))
-        nc.sync.dma_start(q_raw[1][:], q_rows[:, :, HALF:NQ])
 
         ident = held.tile([P, P], F32, name="ident", align_bytes=64)
         make_identity(nc, ident[:])
 
         kn_listed = held.tile([P, N], F32, name="kn_listed", align_bytes=64)
         nc.vector.tensor_copy(kn_listed[:], kn_pool[:].indirect(offsets[:]))
+        k_scale = held.tile([P, N], U8, name="k_scale", align_bytes=64)
+        nc.vector.tensor_copy(k_scale[:], scale_pool[:].indirect(offsets[:]))
 
         qn_ps = psum.tile([P, PACK, P], F32, name="qn_ps", tag="bank6")
         for j in range(PACK):
@@ -69,33 +70,35 @@ def tile_attend_tok_dist_topk_kernel(tc, qT, k_words, k_scales, kn, qn, offs, ou
         for m in range(N // P):
             nc.tensor.transpose(kn_ps[:, m, :], kn_listed[:, m * P : (m + 1) * P], ident[:])
 
-        q_bf = [held.tile([P, HALF, PACK], BF16, name="q_bf%d" % h, align_bytes=64) for h in range(2)]
-        q_codes = [held.tile([P, HALF], U32, name="q_codes%d" % h, align_bytes=64) for h in range(2)]
-        q_scale = [held.tile([P, HALF], U8, name="q_scale%d" % h, align_bytes=64) for h in range(2)]
+        q_bf = held.tile([P, NQ, PACK], BF16, name="q_bf", align_bytes=64)
+        q_codes = held.tile([P, NQ], U32, name="q_codes", align_bytes=64)
+        q_scale = held.tile([P, NQ], U8, name="q_scale", align_bytes=64)
 
-        def views(h, c0, c1):
-            dst = q_bf[h][:, c0:c1, :].rearrange("p (c i) t -> p c t i", i=4)
-            src = q_raw[h][:, :, c0:c1].rearrange("p t (c i) -> p c t i", i=4)
+        def views(raw, first, c0, c1):
+            dst = q_bf[:, c0:c1, :].rearrange("p (c i) t -> p c t i", i=4)
+            src = raw[:, :, c0 - first : c1 - first].rearrange("p t (c i) -> p c t i", i=4)
             return dst, src
 
-        def quantize(h):
+        def quantize(c0, c1):
             nc.vector.quantize_mx(
-                out=q_codes[h][:].bitcast(FP8X4), scales=q_scale[h][:], in_=q_bf[h][:].rearrange("p c t -> p (c t)")
+                out=q_codes[:, c0:c1].bitcast(FP8X4),
+                scales=q_scale[:, c0:c1],
+                in_=q_bf[:, c0:c1, :].rearrange("p c t -> p (c t)"),
             )
 
-        dst, src = views(0, 0, SCALAR_COLS[0])
+        dst, src = views(q_early, 0, EARLY - SCALAR_COLS, NQ // 2)
         nc.scalar.activation(dst, src, COPY, scale=-2.0)
-        dst, src = views(0, SCALAR_COLS[0], HALF)
+        dst, src = views(q_early, 0, NQ // 2, EARLY)
+        nc.scalar.activation(dst, src, COPY, scale=-2.0)
+        dst, src = views(q_early, 0, 0, EARLY - SCALAR_COLS)
         nc.vector.tensor_scalar(dst, src, -2.0, None, MULT)
-        quantize(0)
+        quantize(0, 256)
+        quantize(256, 512)
 
         qn_rows = held.tile([P, NQ], F32, name="qn_rows", align_bytes=64)
         nc.scalar.copy(qn_rows[:].rearrange("p (c j) -> p c j", j=PACK), qn_ps[:].rearrange("p j c -> p c j"))
         kn_cols = held.tile([P, N // P], F32, name="kn_cols", align_bytes=64)
         nc.scalar.copy(kn_cols[:], kn_ps[:, :, KN_ROW])
-
-        k_scale = held.tile([P, N], U8, name="k_scale", align_bytes=64)
-        nc.vector.tensor_copy(k_scale[:], scale_pool[:].indirect(offsets[:]))
 
         k_codes = held.tile([P, N], U32, name="k_codes", align_bytes=64)
         for g in range(2):
@@ -104,32 +107,24 @@ def tile_attend_tok_dist_topk_kernel(tc, qT, k_words, k_scales, kn, qn, offs, ou
                 word_pool[:].indirect(offsets[:, g * N // 32 : (g + 1) * N // 32]),
             )
 
-        dst, src = views(1, 0, SCALAR_COLS[1])
-        nc.scalar.activation(dst, src, COPY, scale=-2.0)
-        nc.gpsimd.tensor_scalar(
-            q_bf[1][:, SCALAR_COLS[1] :, :],
-            q_raw[1][:, :, SCALAR_COLS[1] :].rearrange("p t c -> p c t"),
-            -2.0,
-            0.0,
-            MULT,
-            ADD,
-        )
-        quantize(1)
-
-        for h in range(2):
-            cols = slice(h * HALF, (h + 1) * HALF)
-            for m in range(N // P):
-                slots = slice(m * P, (m + 1) * P)
-                acc = psum.tile([P, HALF], F32, name="acc%d_%d" % (h, m), tag="bank%d" % (4 * h + m))
+        half = NQ // 2
+        for m in range(N // P):
+            slots = slice(m * P, (m + 1) * P)
+            res = held.tile([P, NQ], F32, name="res%d" % m, align_bytes=64)
+            for h in range(2):
+                cols = slice(h * half, (h + 1) * half)
+                acc = psum.tile([P, half], F32, name="acc%d_%d" % (m, h), tag="bank%d" % (2 * m + h))
                 nc.tensor.matmul_mx(
                     out=acc[:],
                     lhsT=k_codes[:, slots].bitcast(FP8X4),
                     lhsT_scale=k_scale[:, slots],
-                    rhs=q_codes[h][:].bitcast(FP8X4),
-                    rhs_scale=q_scale[h][:],
+                    rhs=q_codes[:, cols].bitcast(FP8X4),
+                    rhs_scale=q_scale[:, cols],
                     start=True,
                     stop=True,
                 )
-                res = held.tile([P, HALF], F32, name="res%d_%d" % (h, m), align_bytes=64)
-                nc.vector.scalar_tensor_tensor(res[:], acc[:], kn_cols[:, m : m + 1], qn_rows[:, cols], ADD, ADD)
-                nc.sync.dma_start(out[0, slots, cols], res[:])
+                nc.vector.scalar_tensor_tensor(res[:, cols], acc[:], kn_cols[:, m : m + 1], qn_rows[:, cols], ADD, ADD)
+                if m in (0, N // P - 1):
+                    nc.sync.dma_start(out[0, slots, cols], res[:, cols])
+            if m not in (0, N // P - 1):
+                nc.sync.dma_start(out[0, slots, :], res[:])

@@ -21,7 +21,7 @@ P = 128
 PACK = 4
 KN_ROW = P - 1
 EARLY = 512
-SCALAR_COLS = 352
+SCALAR_COLS = 256
 
 
 def tile_attend_tok_dist_topk_kernel(tc, qT, k_words, k_scales, kn, qn, offs, out):
@@ -36,11 +36,12 @@ def tile_attend_tok_dist_topk_kernel(tc, qT, k_words, k_scales, kn, qn, offs, ou
         scale_pool = held.tile([P, T], U8, name="scale_pool", align_bytes=64)
         kn_pool = held.tile([P, T], F32, name="kn_pool", align_bytes=64)
         word_pool = held.tile([P, T], U32, name="word_pool", align_bytes=64)
-        q_early = held.tile([P, PACK, EARLY], F32, name="q_early", align_bytes=64)
+        q_early = held.tile([P, PACK, EARLY], F32, name="q_early", tag="raw", align_bytes=64)
         qn_cols = held.tile([P, PACK], F32, name="qn_cols", align_bytes=64)
 
         nc.gpsimd.memset(scale_pool[:].bitcast(I32), 0)
-        nc.vector.memset(kn_pool[0:KN_ROW, :], 0.0)
+        nc.vector.memset(kn_pool[0:KN_ROW, 0 : T - 1], 0.0)
+        nc.vector.memset(kn_pool[0:KN_ROW, T - 1 : T], 0.0)
 
         q_rows = qT[0].rearrange("(p j) w -> p j w", j=PACK)
         scale_rows = k_scales[0].rearrange("(q r) t -> r q t", r=4)
@@ -49,10 +50,11 @@ def tile_attend_tok_dist_topk_kernel(tc, qT, k_words, k_scales, kn, qn, offs, ou
             for r in rows:
                 eng.dma_start(scale_pool[r:P:32, :].bitcast(I32), scale_rows[r].bitcast(I32))
 
-        nc.scalar.dma_start(kn_pool[KN_ROW:P, :], kn[0:1, :])
-        nc.scalar.dma_start(qn_cols[:], qn[0, 0].rearrange("(p j) -> p j", j=PACK))
-        nc.sync.dma_start(q_early[:], q_rows[:, :, 0:EARLY])
+        nc.sync.dma_start(kn_pool[KN_ROW:P, :], kn[0:1, :])
+        nc.sync.dma_start(q_early[:, 0:2, :], q_rows[:, 0:2, :])
         load_scales(nc.sync, (0, 1, 2, 3))
+        nc.sync.dma_start(q_early[:, 2:4, :], q_rows[:, 2:4, :])
+        nc.sync.dma_start(qn_cols[:], qn[0, 0].rearrange("(p j) -> p j", j=PACK))
         nc.sync.dma_start(word_pool[:].bitcast(I32), k_words[0].rearrange("p t r -> p (t r)").bitcast(I32))
 
         ident = held.tile([P, P], F32, name="ident", align_bytes=64)
@@ -86,8 +88,6 @@ def tile_attend_tok_dist_topk_kernel(tc, qT, k_words, k_scales, kn, qn, offs, ou
                 in_=q_bf[:, c0:c1, :].rearrange("p c t -> p (c t)"),
             )
 
-        dst, src = views(q_early, 0, EARLY - SCALAR_COLS, NQ // 2)
-        nc.scalar.activation(dst, src, COPY, scale=-2.0)
         dst, src = views(q_early, 0, NQ // 2, EARLY)
         nc.scalar.activation(dst, src, COPY, scale=-2.0)
         dst, src = views(q_early, 0, 0, EARLY - SCALAR_COLS)
@@ -95,17 +95,16 @@ def tile_attend_tok_dist_topk_kernel(tc, qT, k_words, k_scales, kn, qn, offs, ou
         quantize(0, 256)
         quantize(256, 512)
 
-        qn_rows = held.tile([P, NQ], F32, name="qn_rows", align_bytes=64)
+        qn_rows = held.tile([P, NQ], F32, name="qn_rows", tag="raw", align_bytes=64)
         nc.scalar.copy(qn_rows[:].rearrange("p (c j) -> p c j", j=PACK), qn_ps[:].rearrange("p j c -> p c j"))
         kn_cols = held.tile([P, N // P], F32, name="kn_cols", align_bytes=64)
         nc.scalar.copy(kn_cols[:], kn_ps[:, :, KN_ROW])
 
-        k_codes = held.tile([P, N], U32, name="k_codes", align_bytes=64)
+        k_codes = []
         for g in range(2):
-            nc.vector.tensor_copy(
-                k_codes[:, g * N // 2 : (g + 1) * N // 2],
-                word_pool[:].indirect(offsets[:, g * N // 32 : (g + 1) * N // 32]),
-            )
+            part = held.tile([P, N // 2], U32, name="k_codes%d" % g, align_bytes=64)
+            nc.vector.tensor_copy(part[:], word_pool[:].indirect(offsets[:, g * N // 32 : (g + 1) * N // 32]))
+            k_codes.append(part)
 
         half = NQ // 2
         for m in range(N // P):
@@ -116,7 +115,7 @@ def tile_attend_tok_dist_topk_kernel(tc, qT, k_words, k_scales, kn, qn, offs, ou
                 acc = psum.tile([P, half], F32, name="acc%d_%d" % (m, h), tag="bank%d" % (2 * m + h))
                 nc.tensor.matmul_mx(
                     out=acc[:],
-                    lhsT=k_codes[:, slots].bitcast(FP8X4),
+                    lhsT=k_codes[m // 2][:, (m % 2) * P : (m % 2 + 1) * P].bitcast(FP8X4),
                     lhsT_scale=k_scale[:, slots],
                     rhs=q_codes[:, cols].bitcast(FP8X4),
                     rhs_scale=q_scale[:, cols],

@@ -40,8 +40,9 @@ def tile_attend_tok_dist_topk_kernel(tc, qT, k_words, k_scales, kn, qn, offs, ou
         qn_cols = held.tile([P, PACK], F32, name="qn_cols", align_bytes=64)
 
         nc.gpsimd.memset(scale_pool[:].bitcast(I32), 0)
-        nc.vector.memset(kn_pool[0:KN_ROW, 0 : T - 1], 0.0)
-        nc.vector.memset(kn_pool[0:KN_ROW, T - 1 : T], 0.0)
+        nc.vector.memset(kn_pool[0:KN_ROW, 0:639], 0.0)
+        nc.vector.memset(kn_pool[0:KN_ROW, 639:1280], 0.0)
+        nc.gpsimd.memset(kn_pool[0:KN_ROW, 1280:T], 0.0)
 
         q_rows = qT[0].rearrange("(p j) w -> p j w", j=PACK)
         scale_rows = k_scales[0].rearrange("(q r) t -> r q t", r=4)
@@ -65,12 +66,14 @@ def tile_attend_tok_dist_topk_kernel(tc, qT, k_words, k_scales, kn, qn, offs, ou
         k_scale = held.tile([P, N], U8, name="k_scale", align_bytes=64)
         nc.vector.tensor_copy(k_scale[:], scale_pool[:].indirect(offsets[:]))
 
-        qn_ps = psum.tile([P, PACK, P], F32, name="qn_ps", tag="bank6")
-        for j in range(PACK):
-            nc.tensor.transpose(qn_ps[:, j, :], qn_cols[:, j : j + 1].to_broadcast([P, P]), ident[:])
         kn_ps = psum.tile([P, N // P, P], F32, name="kn_ps", tag="bank7")
         for m in range(N // P):
             nc.tensor.transpose(kn_ps[:, m, :], kn_listed[:, m * P : (m + 1) * P], ident[:])
+        kn_cols = held.tile([P, N // P], F32, name="kn_cols", align_bytes=64)
+        nc.scalar.copy(kn_cols[:], kn_ps[:, :, KN_ROW])
+        qn_ps = psum.tile([P, PACK, P], F32, name="qn_ps", tag="bank6")
+        for j in range(PACK):
+            nc.tensor.transpose(qn_ps[:, j, :], qn_cols[:, j : j + 1].to_broadcast([P, P]), ident[:])
 
         q_bf = held.tile([P, NQ, PACK], BF16, name="q_bf", align_bytes=64)
         q_codes = held.tile([P, NQ], U32, name="q_codes", align_bytes=64)
@@ -89,16 +92,15 @@ def tile_attend_tok_dist_topk_kernel(tc, qT, k_words, k_scales, kn, qn, offs, ou
             )
 
         dst, src = views(q_early, 0, NQ // 2, EARLY)
-        nc.scalar.activation(dst, src, COPY, scale=-2.0)
+        for t in (0, 2):
+            nc.scalar.activation(dst[:, :, t : t + 2, :], src[:, :, t : t + 2, :], COPY, scale=-2.0)
         dst, src = views(q_early, 0, 0, EARLY - SCALAR_COLS)
         nc.vector.tensor_scalar(dst, src, -2.0, None, MULT)
-        quantize(0, 256)
         quantize(256, 512)
+        quantize(0, 256)
 
         qn_rows = held.tile([P, NQ], F32, name="qn_rows", tag="raw", align_bytes=64)
         nc.scalar.copy(qn_rows[:].rearrange("p (c j) -> p c j", j=PACK), qn_ps[:].rearrange("p j c -> p c j"))
-        kn_cols = held.tile([P, N // P], F32, name="kn_cols", align_bytes=64)
-        nc.scalar.copy(kn_cols[:], kn_ps[:, :, KN_ROW])
 
         k_codes = []
         for g in range(2):

@@ -16,12 +16,14 @@ FP8X4 = mybir.dt.float8_e4m3fn_x4
 ADD = mybir.AluOpType.add
 MULT = mybir.AluOpType.mult
 COPY = mybir.ActivationFunctionType.Copy
+IDENT = mybir.ActivationFunctionType.Identity
 
 P = 128
 PACK = 4
 KN_ROW = P - 1
-EARLY = 512
-SCALAR_COLS = 256
+HALF = NQ // 2
+SCALE_ROW0 = 48
+VECTOR_COLS = 320
 
 
 def tile_attend_tok_dist_topk_kernel(tc, qT, k_words, k_scales, kn, qn, offs, out):
@@ -36,52 +38,48 @@ def tile_attend_tok_dist_topk_kernel(tc, qT, k_words, k_scales, kn, qn, offs, ou
         scale_pool = held.tile([P, T], U8, name="scale_pool", align_bytes=64)
         kn_pool = held.tile([P, T], F32, name="kn_pool", align_bytes=64)
         word_pool = held.tile([P, T], U32, name="word_pool", align_bytes=64)
-        q_early = held.tile([P, PACK, EARLY], F32, name="q_early", tag="raw", align_bytes=64)
+        q_raw = held.tile([P, PACK, NQ], F32, name="q_raw", tag="raw", align_bytes=64)
         qn_cols = held.tile([P, PACK], F32, name="qn_cols", align_bytes=64)
+        k_scale = held.tile([P, N], U8, name="k_scale", align_bytes=64)
+        ident = held.tile([P, P], F32, name="ident", align_bytes=64)
 
-        nc.gpsimd.memset(scale_pool[:].bitcast(I32), 0)
-        nc.vector.memset(kn_pool[0:KN_ROW, 0:639], 0.0)
-        nc.vector.memset(kn_pool[0:KN_ROW, 639:1280], 0.0)
-        nc.gpsimd.memset(kn_pool[0:KN_ROW, 1280:T], 0.0)
-
-        q_rows = qT[0].rearrange("(p j) w -> p j w", j=PACK)
-        scale_rows = k_scales[0].rearrange("(q r) t -> r q t", r=4)
-
-        def load_scales(eng, rows):
-            for r in rows:
-                eng.dma_start(scale_pool[r:P:32, :].bitcast(I32), scale_rows[r].bitcast(I32))
-
+        nc.scalar.dma_start(scale_pool[SCALE_ROW0 : SCALE_ROW0 + 16, :].bitcast(I32), k_scales[0].bitcast(I32))
+        nc.scalar.dma_start(qn_cols[:], qn[0, 0].rearrange("(p j) -> p j", j=PACK))
         nc.sync.dma_start(kn_pool[KN_ROW:P, :], kn[0:1, :])
-        nc.sync.dma_start(q_early[:, 0:2, :], q_rows[:, 0:2, :])
-        load_scales(nc.sync, (0, 1, 2, 3))
-        nc.sync.dma_start(q_early[:, 2:4, :], q_rows[:, 2:4, :])
-        nc.sync.dma_start(qn_cols[:], qn[0, 0].rearrange("(p j) -> p j", j=PACK))
+        nc.sync.dma_start(q_raw[:], qT[0].rearrange("(p j) w -> p j w", j=PACK))
         nc.sync.dma_start(word_pool[:].bitcast(I32), k_words[0].rearrange("p t r -> p (t r)").bitcast(I32))
 
-        ident = held.tile([P, P], F32, name="ident", align_bytes=64)
+        nc.vector.memset(scale_pool[0:SCALE_ROW0, :].bitcast(I32), 0)
+        nc.gpsimd.memset(scale_pool[SCALE_ROW0 + 16 : P, :].bitcast(I32), 0)
+        nc.vector.memset(kn_pool[0:KN_ROW, 0 : T // 2], 0.0)
+        nc.gpsimd.memset(k_scale[:].bitcast(I32), 0)
         make_identity(nc, ident[:])
+        nc.gpsimd.memset(kn_pool[0:KN_ROW, T // 2 : T], 0.0)
 
+        scale_listed = held.tile([P, N], U8, name="scale_listed", align_bytes=64)
+        nc.vector.tensor_copy(scale_listed[:], scale_pool[:].indirect(offsets[:]))
+        for g in range(4):
+            rows = scale_listed[SCALE_ROW0 + 4 * g : SCALE_ROW0 + 4 * g + 4, :]
+            nc.sync.dma_start(k_scale[32 * g : 32 * g + 4, :].bitcast(I32), rows.bitcast(I32))
         kn_listed = held.tile([P, N], F32, name="kn_listed", align_bytes=64)
         nc.vector.tensor_copy(kn_listed[:], kn_pool[:].indirect(offsets[:]))
-        k_scale = held.tile([P, N], U8, name="k_scale", align_bytes=64)
-        nc.vector.tensor_copy(k_scale[:], scale_pool[:].indirect(offsets[:]))
 
-        kn_ps = psum.tile([P, N // P, P], F32, name="kn_ps", tag="bank7")
-        for m in range(N // P):
-            nc.tensor.transpose(kn_ps[:, m, :], kn_listed[:, m * P : (m + 1) * P], ident[:])
-        kn_cols = held.tile([P, N // P], F32, name="kn_cols", align_bytes=64)
-        nc.scalar.copy(kn_cols[:], kn_ps[:, :, KN_ROW])
         qn_ps = psum.tile([P, PACK, P], F32, name="qn_ps", tag="bank6")
         for j in range(PACK):
             nc.tensor.transpose(qn_ps[:, j, :], qn_cols[:, j : j + 1].to_broadcast([P, P]), ident[:])
+        kn_ps = psum.tile([P, N // P, P], F32, name="kn_ps", tag="bank7")
+        for m in range(N // P):
+            nc.tensor.transpose(kn_ps[:, m, :], kn_listed[:, m * P : (m + 1) * P], ident[:])
+        qn_rows = held.tile([P, NQ], F32, name="qn_rows", align_bytes=64)
+        nc.scalar.copy(qn_rows[:].rearrange("p (c j) -> p c j", j=PACK), qn_ps[:].rearrange("p j c -> p c j"))
 
-        q_bf = held.tile([P, NQ, PACK], BF16, name="q_bf", align_bytes=64)
+        q_bf = held.tile([P, NQ, PACK], BF16, name="q_bf", tag="q_bf", align_bytes=64)
         q_codes = held.tile([P, NQ], U32, name="q_codes", align_bytes=64)
         q_scale = held.tile([P, NQ], U8, name="q_scale", align_bytes=64)
 
-        def views(raw, first, c0, c1):
+        def views(c0, c1):
             dst = q_bf[:, c0:c1, :].rearrange("p (c i) t -> p c t i", i=4)
-            src = raw[:, :, c0 - first : c1 - first].rearrange("p t (c i) -> p c t i", i=4)
+            src = q_raw[:, :, c0:c1].rearrange("p t (c i) -> p c t i", i=4)
             return dst, src
 
         def quantize(c0, c1):
@@ -91,30 +89,45 @@ def tile_attend_tok_dist_topk_kernel(tc, qT, k_words, k_scales, kn, qn, offs, ou
                 in_=q_bf[:, c0:c1, :].rearrange("p c t -> p (c t)"),
             )
 
-        dst, src = views(q_early, 0, NQ // 2, EARLY)
-        for t in (0, 2):
-            nc.scalar.activation(dst[:, :, t : t + 2, :], src[:, :, t : t + 2, :], COPY, scale=-2.0)
-        dst, src = views(q_early, 0, 0, EARLY - SCALAR_COLS)
+        dst, src = views(VECTOR_COLS, NQ)
+        nc.scalar.activation(dst, src, COPY, scale=-2.0)
+        dst, src = views(0, VECTOR_COLS)
         nc.vector.tensor_scalar(dst, src, -2.0, None, MULT)
-        quantize(256, 512)
-        quantize(0, 256)
+        quantize(0, HALF)
+        quantize(HALF, NQ)
 
-        qn_rows = held.tile([P, NQ], F32, name="qn_rows", tag="raw", align_bytes=64)
-        nc.scalar.copy(qn_rows[:].rearrange("p (c j) -> p c j", j=PACK), qn_ps[:].rearrange("p j c -> p c j"))
+        kn_cols = held.tile([P, N // P], F32, name="kn_cols", align_bytes=64)
+        nc.scalar.copy(kn_cols[:], kn_ps[:, :, KN_ROW])
 
+        warm = psum.tile([P, HALF], F32, name="warm", tag="bank7")
+        nc.tensor.matmul_mx(
+            out=warm[:],
+            lhsT=q_codes[:, 0:P].bitcast(FP8X4),
+            lhsT_scale=k_scale[:, 0:P],
+            rhs=q_codes[:, 0:HALF].bitcast(FP8X4),
+            rhs_scale=q_scale[:, 0:HALF],
+            start=True,
+            stop=True,
+        )
         k_codes = []
+        listed = held.tile([P, N], U32, name="listed", tag="q_bf", align_bytes=64)
         for g in range(2):
-            part = held.tile([P, N // 2], U32, name="k_codes%d" % g, align_bytes=64)
-            nc.vector.tensor_copy(part[:], word_pool[:].indirect(offsets[:, g * N // 32 : (g + 1) * N // 32]))
+            part = listed[:, g * N // 2 : (g + 1) * N // 2]
+            nc.vector.tensor_copy(part, word_pool[:].indirect(offsets[:, g * N // 32 : (g + 1) * N // 32]))
             k_codes.append(part)
 
-        half = NQ // 2
+        pieces = ((256, 256), (256, 256), (256, 256), (256, 256))
+        stores = ((256, 512), (512,), (512,), (256, 512))
+        bank = 0
         for m in range(N // P):
             slots = slice(m * P, (m + 1) * P)
             res = held.tile([P, NQ], F32, name="res%d" % m, align_bytes=64)
-            for h in range(2):
-                cols = slice(h * half, (h + 1) * half)
-                acc = psum.tile([P, half], F32, name="acc%d_%d" % (m, h), tag="bank%d" % (2 * m + h))
+            c0 = 0
+            s0 = 0
+            for width in pieces[m]:
+                cols = slice(c0, c0 + width)
+                acc = psum.tile([P, width], F32, name="acc%d_%d" % (m, c0), tag="bank%d" % (bank % 8))
+                bank = bank + 1
                 nc.tensor.matmul_mx(
                     out=acc[:],
                     lhsT=k_codes[m // 2][:, (m % 2) * P : (m % 2 + 1) * P].bitcast(FP8X4),
@@ -125,7 +138,7 @@ def tile_attend_tok_dist_topk_kernel(tc, qT, k_words, k_scales, kn, qn, offs, ou
                     stop=True,
                 )
                 nc.vector.scalar_tensor_tensor(res[:, cols], acc[:], kn_cols[:, m : m + 1], qn_rows[:, cols], ADD, ADD)
-                if m in (0, N // P - 1):
-                    nc.sync.dma_start(out[0, slots, cols], res[:, cols])
-            if m not in (0, N // P - 1):
-                nc.sync.dma_start(out[0, slots, :], res[:])
+                c0 = c0 + width
+                if c0 in stores[m]:
+                    nc.sync.dma_start(out[0, slots, s0:c0], res[:, s0:c0])
+                    s0 = c0

@@ -24,6 +24,7 @@ KN_ROW = P - 1
 HALF = NQ // 2
 SCALE_ROW0 = 48
 VECTOR_COLS = 320
+EARLY_WORDS = 1536
 
 
 def tile_attend_tok_dist_topk_kernel(tc, qT, k_words, k_scales, kn, qn, offs, out):
@@ -46,21 +47,25 @@ def tile_attend_tok_dist_topk_kernel(tc, qT, k_words, k_scales, kn, qn, offs, ou
         nc.scalar.dma_start(scale_pool[SCALE_ROW0 : SCALE_ROW0 + 16, :].bitcast(I32), k_scales[0].bitcast(I32))
         nc.scalar.dma_start(qn_cols[:], qn[0, 0].rearrange("(p j) -> p j", j=PACK))
         nc.sync.dma_start(kn_pool[KN_ROW:P, :], kn[0:1, :])
-        nc.sync.dma_start(q_raw[:], qT[0].rearrange("(p j) w -> p j w", j=PACK))
-        nc.sync.dma_start(word_pool[:].bitcast(I32), k_words[0].rearrange("p t r -> p (t r)").bitcast(I32))
+        q_rows = qT[0].rearrange("(p j) w -> p j w", j=PACK)
+        words = k_words[0].rearrange("p t r -> p (t r)").bitcast(I32)
+        nc.sync.dma_start(q_raw[:], q_rows)
+        nc.sync.dma_start(word_pool[:, 0:EARLY_WORDS].bitcast(I32), words[:, 0:EARLY_WORDS])
 
-        nc.vector.memset(scale_pool[0:SCALE_ROW0, :].bitcast(I32), 0)
+        nc.gpsimd.memset(scale_pool[0:SCALE_ROW0, :].bitcast(I32), 0)
         nc.gpsimd.memset(scale_pool[SCALE_ROW0 + 16 : P, :].bitcast(I32), 0)
-        nc.vector.memset(kn_pool[0:KN_ROW, 0 : T // 2], 0.0)
+        nc.vector.memset(kn_pool[0:KN_ROW, 0:767], 0.0)
+        nc.vector.memset(kn_pool[0:KN_ROW, 767:1536], 0.0)
+        nc.gpsimd.memset(kn_pool[0:KN_ROW, 1536:T], 0.0)
         nc.gpsimd.memset(k_scale[:].bitcast(I32), 0)
         make_identity(nc, ident[:])
-        nc.gpsimd.memset(kn_pool[0:KN_ROW, T // 2 : T], 0.0)
 
         scale_listed = held.tile([P, N], U8, name="scale_listed", align_bytes=64)
         nc.vector.tensor_copy(scale_listed[:], scale_pool[:].indirect(offsets[:]))
         for g in range(4):
             rows = scale_listed[SCALE_ROW0 + 4 * g : SCALE_ROW0 + 4 * g + 4, :]
             nc.sync.dma_start(k_scale[32 * g : 32 * g + 4, :].bitcast(I32), rows.bitcast(I32))
+        nc.sync.dma_start(word_pool[:, EARLY_WORDS:T].bitcast(I32), words[:, EARLY_WORDS:T])
         kn_listed = held.tile([P, N], F32, name="kn_listed", align_bytes=64)
         nc.vector.tensor_copy(kn_listed[:], kn_pool[:].indirect(offsets[:]))
 
@@ -91,21 +96,22 @@ def tile_attend_tok_dist_topk_kernel(tc, qT, k_words, k_scales, kn, qn, offs, ou
 
         dst, src = views(VECTOR_COLS, NQ)
         nc.scalar.activation(dst, src, COPY, scale=-2.0)
-        dst, src = views(0, VECTOR_COLS)
-        nc.vector.tensor_scalar(dst, src, -2.0, None, MULT)
+        for c0, c1 in ((0, HALF), (HALF, VECTOR_COLS)):
+            dst, src = views(c0, c1)
+            nc.vector.tensor_scalar(dst, src, -2.0, None, MULT)
         quantize(0, HALF)
         quantize(HALF, NQ)
 
         kn_cols = held.tile([P, N // P], F32, name="kn_cols", align_bytes=64)
         nc.scalar.copy(kn_cols[:], kn_ps[:, :, KN_ROW])
 
-        warm = psum.tile([P, HALF], F32, name="warm", tag="bank7")
+        warm = psum.tile([P, NQ], F32, name="warm", tag="bank7")
         nc.tensor.matmul_mx(
             out=warm[:],
             lhsT=q_codes[:, 0:P].bitcast(FP8X4),
             lhsT_scale=k_scale[:, 0:P],
-            rhs=q_codes[:, 0:HALF].bitcast(FP8X4),
-            rhs_scale=q_scale[:, 0:HALF],
+            rhs=q_codes[:].bitcast(FP8X4),
+            rhs_scale=q_scale[:],
             start=True,
             stop=True,
         )
@@ -116,8 +122,8 @@ def tile_attend_tok_dist_topk_kernel(tc, qT, k_words, k_scales, kn, qn, offs, ou
             nc.vector.tensor_copy(part, word_pool[:].indirect(offsets[:, g * N // 32 : (g + 1) * N // 32]))
             k_codes.append(part)
 
-        pieces = ((256, 256), (256, 256), (256, 256), (256, 256))
-        stores = ((256, 512), (512,), (512,), (256, 512))
+        pieces = ((128, 128, 256), (256, 256), (256, 256), (256, 256))
+        stores = ((128, 512), (512,), (512,), (512,))
         bank = 0
         for m in range(N // P):
             slots = slice(m * P, (m + 1) * P)

@@ -24,7 +24,7 @@ KN_ROW = P - 1
 HALF = NQ // 2
 SCALE_ROW0 = 48
 VECTOR_COLS = 320
-EARLY_WORDS = 1536
+EARLY_WORDS = 1792
 
 
 def tile_attend_tok_dist_topk_kernel(tc, qT, k_words, k_scales, kn, qn, offs, out):
@@ -44,19 +44,19 @@ def tile_attend_tok_dist_topk_kernel(tc, qT, k_words, k_scales, kn, qn, offs, ou
         k_scale = held.tile([P, N], U8, name="k_scale", align_bytes=64)
         ident = held.tile([P, P], F32, name="ident", align_bytes=64)
 
-        nc.scalar.dma_start(scale_pool[SCALE_ROW0 : SCALE_ROW0 + 16, :].bitcast(I32), k_scales[0].bitcast(I32))
-        nc.scalar.dma_start(qn_cols[:], qn[0, 0].rearrange("(p j) -> p j", j=PACK))
+        nc.sync.dma_start(scale_pool[SCALE_ROW0 : SCALE_ROW0 + 16, :].bitcast(I32), k_scales[0].bitcast(I32))
         nc.sync.dma_start(kn_pool[KN_ROW:P, :], kn[0:1, :])
         q_rows = qT[0].rearrange("(p j) w -> p j w", j=PACK)
         words = k_words[0].rearrange("p t r -> p (t r)").bitcast(I32)
         nc.sync.dma_start(q_raw[:], q_rows)
+        nc.sync.dma_start(qn_cols[:], qn[0, 0].rearrange("(p j) -> p j", j=PACK))
         nc.sync.dma_start(word_pool[:, 0:EARLY_WORDS].bitcast(I32), words[:, 0:EARLY_WORDS])
 
         nc.gpsimd.memset(scale_pool[0:SCALE_ROW0, :].bitcast(I32), 0)
         nc.gpsimd.memset(scale_pool[SCALE_ROW0 + 16 : P, :].bitcast(I32), 0)
-        nc.vector.memset(kn_pool[0:KN_ROW, 0:767], 0.0)
-        nc.vector.memset(kn_pool[0:KN_ROW, 767:1536], 0.0)
-        nc.gpsimd.memset(kn_pool[0:KN_ROW, 1536:T], 0.0)
+        nc.vector.memset(kn_pool[0:KN_ROW, 0:895], 0.0)
+        nc.vector.memset(kn_pool[0:KN_ROW, 895:1792], 0.0)
+        nc.gpsimd.memset(kn_pool[0:KN_ROW, 1792:T], 0.0)
         nc.gpsimd.memset(k_scale[:].bitcast(I32), 0)
         make_identity(nc, ident[:])
 

@@ -105,16 +105,6 @@ def tile_attend_tok_dist_topk_kernel(tc, qT, k_words, k_scales, kn, qn, offs, ou
         kn_cols = held.tile([P, N // P], F32, name="kn_cols", align_bytes=64)
         nc.scalar.copy(kn_cols[:], kn_ps[:, :, KN_ROW])
 
-        warm = psum.tile([P, NQ], F32, name="warm", tag="bank7")
-        nc.tensor.matmul_mx(
-            out=warm[:],
-            lhsT=q_codes[:, 0:P].bitcast(FP8X4),
-            lhsT_scale=k_scale[:, 0:P],
-            rhs=q_codes[:].bitcast(FP8X4),
-            rhs_scale=q_scale[:],
-            start=True,
-            stop=True,
-        )
         k_codes = []
         listed = held.tile([P, N], U32, name="listed", tag="q_bf", align_bytes=64)
         for g in range(2):

@@ -23,8 +23,7 @@ PACK = 4
 KN_ROW = P - 1
 HALF = NQ // 2
 SCALE_ROW0 = 48
-VECTOR_COLS = 320
-EARLY_WORDS = 1792
+SCALAR_COLS = 128
 
 
 def tile_attend_tok_dist_topk_kernel(tc, qT, k_words, k_scales, kn, qn, offs, out):
@@ -36,10 +35,10 @@ def tile_attend_tok_dist_topk_kernel(tc, qT, k_words, k_scales, kn, qn, offs, ou
         offsets = held.tile([P, N // 16], U16, name="offsets")
         nc.sync.dma_start(offsets[:], offs)
 
-        scale_pool = held.tile([P, T], U8, name="scale_pool", align_bytes=64)
+        scale_pool = held.tile([P, T], U8, name="scale_pool", tag="scale_pool", align_bytes=64)
         kn_pool = held.tile([P, T], F32, name="kn_pool", align_bytes=64)
         word_pool = held.tile([P, T], U32, name="word_pool", align_bytes=64)
-        q_raw = held.tile([P, PACK, NQ], F32, name="q_raw", tag="raw", align_bytes=64)
+        q_early = held.tile([P, PACK, HALF], F32, name="q_early", align_bytes=64)
         qn_cols = held.tile([P, PACK], F32, name="qn_cols", align_bytes=64)
         k_scale = held.tile([P, N], U8, name="k_scale", align_bytes=64)
         ident = held.tile([P, P], F32, name="ident", align_bytes=64)
@@ -48,9 +47,9 @@ def tile_attend_tok_dist_topk_kernel(tc, qT, k_words, k_scales, kn, qn, offs, ou
         nc.sync.dma_start(kn_pool[KN_ROW:P, :], kn[0:1, :])
         q_rows = qT[0].rearrange("(p j) w -> p j w", j=PACK)
         words = k_words[0].rearrange("p t r -> p (t r)").bitcast(I32)
-        nc.sync.dma_start(q_raw[:], q_rows)
+        nc.sync.dma_start(q_early[:], q_rows[:, :, 0:HALF])
         nc.sync.dma_start(qn_cols[:], qn[0, 0].rearrange("(p j) -> p j", j=PACK))
-        nc.sync.dma_start(word_pool[:, 0:EARLY_WORDS].bitcast(I32), words[:, 0:EARLY_WORDS])
+        nc.sync.dma_start(word_pool[:].bitcast(I32), words)
 
         nc.gpsimd.memset(scale_pool[0:SCALE_ROW0, :].bitcast(I32), 0)
         nc.gpsimd.memset(scale_pool[SCALE_ROW0 + 16 : P, :].bitcast(I32), 0)
@@ -65,9 +64,31 @@ def tile_attend_tok_dist_topk_kernel(tc, qT, k_words, k_scales, kn, qn, offs, ou
         for g in range(4):
             rows = scale_listed[SCALE_ROW0 + 4 * g : SCALE_ROW0 + 4 * g + 4, :]
             nc.sync.dma_start(k_scale[32 * g : 32 * g + 4, :].bitcast(I32), rows.bitcast(I32))
-        nc.sync.dma_start(word_pool[:, EARLY_WORDS:T].bitcast(I32), words[:, EARLY_WORDS:T])
+        q_late = held.tile([P, PACK, HALF], F32, name="q_late", tag="scale_pool", align_bytes=64)
+        nc.sync.dma_start(q_late[:, 0:2, :], q_rows[:, 0:2, HALF:NQ])
+        nc.sync.dma_start(q_late[:, 2:4, :], q_rows[:, 2:4, HALF:NQ])
         kn_listed = held.tile([P, N], F32, name="kn_listed", align_bytes=64)
         nc.vector.tensor_copy(kn_listed[:], kn_pool[:].indirect(offsets[:]))
+
+        bf_early = held.tile([P, HALF, PACK], BF16, name="bf_early", tag="bf_early", align_bytes=64)
+        bf_late = held.tile([P, HALF, PACK], BF16, name="bf_late", tag="bf_late", align_bytes=64)
+        q_codes = [held.tile([P, HALF], U32, name="q_codes%d" % h, align_bytes=64) for h in range(2)]
+        q_scale = [held.tile([P, HALF], U8, name="q_scale%d" % h, align_bytes=64) for h in range(2)]
+
+        def cast(dst, src):
+            nc.scalar.activation(
+                dst.rearrange("p (c i) t -> p c t i", i=4), src.rearrange("p t (c i) -> p c t i", i=4), COPY, scale=-2.0
+            )
+
+        def quantize(h, bf):
+            nc.vector.quantize_mx(
+                out=q_codes[h][:].bitcast(FP8X4),
+                scales=q_scale[h][:],
+                in_=bf[:].rearrange("p c t -> p (c t)"),
+            )
+
+        cast(bf_early[:], q_early[:])
+        quantize(0, bf_early)
 
         qn_ps = psum.tile([P, PACK, P], F32, name="qn_ps", tag="bank6")
         for j in range(PACK):
@@ -77,64 +98,45 @@ def tile_attend_tok_dist_topk_kernel(tc, qT, k_words, k_scales, kn, qn, offs, ou
             nc.tensor.transpose(kn_ps[:, m, :], kn_listed[:, m * P : (m + 1) * P], ident[:])
         qn_rows = held.tile([P, NQ], F32, name="qn_rows", align_bytes=64)
         nc.scalar.copy(qn_rows[:].rearrange("p (c j) -> p c j", j=PACK), qn_ps[:].rearrange("p j c -> p c j"))
-
-        q_bf = held.tile([P, NQ, PACK], BF16, name="q_bf", tag="q_bf", align_bytes=64)
-        q_codes = held.tile([P, NQ], U32, name="q_codes", align_bytes=64)
-        q_scale = held.tile([P, NQ], U8, name="q_scale", align_bytes=64)
-
-        def views(c0, c1):
-            dst = q_bf[:, c0:c1, :].rearrange("p (c i) t -> p c t i", i=4)
-            src = q_raw[:, :, c0:c1].rearrange("p t (c i) -> p c t i", i=4)
-            return dst, src
-
-        def quantize(c0, c1):
-            nc.vector.quantize_mx(
-                out=q_codes[:, c0:c1].bitcast(FP8X4),
-                scales=q_scale[:, c0:c1],
-                in_=q_bf[:, c0:c1, :].rearrange("p c t -> p (c t)"),
-            )
-
-        dst, src = views(VECTOR_COLS, NQ)
-        nc.scalar.activation(dst, src, COPY, scale=-2.0)
-        for c0, c1 in ((0, HALF), (HALF, VECTOR_COLS)):
-            dst, src = views(c0, c1)
-            nc.vector.tensor_scalar(dst, src, -2.0, None, MULT)
-        quantize(0, HALF)
-        quantize(HALF, NQ)
-
         kn_cols = held.tile([P, N // P], F32, name="kn_cols", align_bytes=64)
         nc.scalar.copy(kn_cols[:], kn_ps[:, :, KN_ROW])
 
-        k_codes = []
-        listed = held.tile([P, N], U32, name="listed", tag="q_bf", align_bytes=64)
+        listed = held.tile([P, N], U32, name="listed", tag="bf_early", align_bytes=64)
         for g in range(2):
             part = listed[:, g * N // 2 : (g + 1) * N // 2]
             nc.vector.tensor_copy(part, word_pool[:].indirect(offsets[:, g * N // 32 : (g + 1) * N // 32]))
-            k_codes.append(part)
 
-        pieces = ((128, 128, 256), (256, 256), (256, 256), (256, 256))
-        stores = ((128, 512), (512,), (512,), (512,))
-        bank = 0
-        for m in range(N // P):
+        cast(bf_late[:, :, 0:2], q_late[:, 0:2, :])
+        cast(bf_late[:, 0:SCALAR_COLS, 2:4], q_late[:, 2:4, 0:SCALAR_COLS])
+        nc.gpsimd.tensor_scalar(
+            bf_late[:, SCALAR_COLS:HALF, 2:4],
+            q_late[:, 2:4, SCALAR_COLS:HALF].rearrange("p t c -> p c t"),
+            -2.0,
+            0.0,
+            MULT,
+            ADD,
+        )
+
+        def piece(h, m, tag):
             slots = slice(m * P, (m + 1) * P)
-            res = held.tile([P, NQ], F32, name="res%d" % m, align_bytes=64)
-            c0 = 0
-            s0 = 0
-            for width in pieces[m]:
-                cols = slice(c0, c0 + width)
-                acc = psum.tile([P, width], F32, name="acc%d_%d" % (m, c0), tag="bank%d" % (bank % 8))
-                bank = bank + 1
-                nc.tensor.matmul_mx(
-                    out=acc[:],
-                    lhsT=k_codes[m // 2][:, (m % 2) * P : (m % 2 + 1) * P].bitcast(FP8X4),
-                    lhsT_scale=k_scale[:, slots],
-                    rhs=q_codes[:, cols].bitcast(FP8X4),
-                    rhs_scale=q_scale[:, cols],
-                    start=True,
-                    stop=True,
-                )
-                nc.vector.scalar_tensor_tensor(res[:, cols], acc[:], kn_cols[:, m : m + 1], qn_rows[:, cols], ADD, ADD)
-                c0 = c0 + width
-                if c0 in stores[m]:
-                    nc.sync.dma_start(out[0, slots, s0:c0], res[:, s0:c0])
-                    s0 = c0
+            cols = slice(h * HALF, (h + 1) * HALF)
+            res = held.tile([P, HALF], F32, name="res%d_%d" % (h, m), tag=tag, align_bytes=64)
+            acc = psum.tile([P, HALF], F32, name="acc%d_%d" % (h, m), tag="bank%d" % (4 * h + m))
+            nc.tensor.matmul_mx(
+                out=acc[:],
+                lhsT=listed[:, slots].bitcast(FP8X4),
+                lhsT_scale=k_scale[:, slots],
+                rhs=q_codes[h][:].bitcast(FP8X4),
+                rhs_scale=q_scale[h][:],
+                start=True,
+                stop=True,
+            )
+            nc.vector.scalar_tensor_tensor(res[:], acc[:], kn_cols[:, m : m + 1], qn_rows[:, cols], ADD, ADD)
+            nc.sync.dma_start(out[0, slots, cols], res[:])
+
+        for m in range(3):
+            piece(0, m, "res0_%d" % m)
+        quantize(1, bf_late)
+        piece(0, 3, "bf_late")
+        for m in range(4):
+            piece(1, m, "res1_%d" % m)

@@ -23,7 +23,7 @@ PACK = 4
 KN_ROW = P - 1
 HALF = NQ // 2
 SCALE_ROW0 = 48
-SCALAR_COLS = 128
+SCALAR_COLS = (176, 144)
 
 
 def tile_attend_tok_dist_topk_kernel(tc, qT, k_words, k_scales, kn, qn, offs, out):
@@ -106,21 +106,21 @@ def tile_attend_tok_dist_topk_kernel(tc, qT, k_words, k_scales, kn, qn, offs, ou
             part = listed[:, g * N // 2 : (g + 1) * N // 2]
             nc.vector.tensor_copy(part, word_pool[:].indirect(offsets[:, g * N // 32 : (g + 1) * N // 32]))
 
-        cast(bf_late[:, :, 0:2], q_late[:, 0:2, :])
-        cast(bf_late[:, 0:SCALAR_COLS, 2:4], q_late[:, 2:4, 0:SCALAR_COLS])
-        nc.gpsimd.tensor_scalar(
-            bf_late[:, SCALAR_COLS:HALF, 2:4],
-            q_late[:, 2:4, SCALAR_COLS:HALF].rearrange("p t c -> p c t"),
-            -2.0,
-            0.0,
-            MULT,
-            ADD,
-        )
+        for pair, split in enumerate(SCALAR_COLS):
+            planes = slice(2 * pair, 2 * pair + 2)
+            cast(bf_late[:, 0:split, planes], q_late[:, planes, 0:split])
+            nc.gpsimd.tensor_scalar(
+                bf_late[:, split:HALF, planes],
+                q_late[:, planes, split:HALF].rearrange("p t c -> p c t"),
+                -2.0,
+                0.0,
+                MULT,
+                ADD,
+            )
 
-        def piece(h, m, tag):
+        def piece(h, m, res):
             slots = slice(m * P, (m + 1) * P)
             cols = slice(h * HALF, (h + 1) * HALF)
-            res = held.tile([P, HALF], F32, name="res%d_%d" % (h, m), tag=tag, align_bytes=64)
             acc = psum.tile([P, HALF], F32, name="acc%d_%d" % (h, m), tag="bank%d" % (4 * h + m))
             nc.tensor.matmul_mx(
                 out=acc[:],
@@ -131,12 +131,16 @@ def tile_attend_tok_dist_topk_kernel(tc, qT, k_words, k_scales, kn, qn, offs, ou
                 start=True,
                 stop=True,
             )
-            nc.vector.scalar_tensor_tensor(res[:], acc[:], kn_cols[:, m : m + 1], qn_rows[:, cols], ADD, ADD)
-            nc.sync.dma_start(out[0, slots, cols], res[:])
+            nc.vector.scalar_tensor_tensor(res, acc[:], kn_cols[:, m : m + 1], qn_rows[:, cols], ADD, ADD)
+            nc.sync.dma_start(out[0, slots, cols], res)
 
-        for m in range(3):
-            piece(0, m, "res0_%d" % m)
+        first = [held.tile([P, HALF], F32, name="first%d" % m, align_bytes=64) for m in range(2)]
+        for m in range(2):
+            piece(0, m, first[m][:])
         quantize(1, bf_late)
-        piece(0, 3, "bf_late")
+        second = held.tile([P, 2 * HALF], F32, name="second", tag="bf_late", align_bytes=64)
+        for m in range(2):
+            piece(0, 2 + m, second[:, m * HALF : (m + 1) * HALF])
         for m in range(4):
-            piece(1, m, "res1_%d" % m)
+            last = held.tile([P, HALF], F32, name="last%d" % m, align_bytes=64)
+            piece(1, m, last[:])

@@ -44,10 +44,10 @@ def tile_attend_tok_dist_topk_kernel(tc, qT, k_words, k_scales, kn, qn, offs, ou
         ident = held.tile([P, P], F32, name="ident", align_bytes=64)
 
         nc.sync.dma_start(scale_pool[SCALE_ROW0 : SCALE_ROW0 + 16, :].bitcast(I32), k_scales[0].bitcast(I32))
-        nc.sync.dma_start(kn_pool[KN_ROW:P, :], kn[0:1, :])
         q_rows = qT[0].rearrange("(p j) w -> p j w", j=PACK)
         words = k_words[0].rearrange("p t r -> p (t r)").bitcast(I32)
         nc.sync.dma_start(q_early[:], q_rows[:, :, 0:HALF])
+        nc.sync.dma_start(kn_pool[KN_ROW:P, :], kn[0:1, :])
         nc.sync.dma_start(qn_cols[:], qn[0, 0].rearrange("(p j) -> p j", j=PACK))
         nc.sync.dma_start(word_pool[:].bitcast(I32), words)
 

@@ -23,7 +23,8 @@ PACK = 4
 KN_ROW = P - 1
 HALF = NQ // 2
 SCALE_ROW0 = 48
-SCALAR_COLS = (176, 144)
+SCALAR_COLS = (176, 176)
+QUARTER = NQ // 4
 
 
 def tile_attend_tok_dist_topk_kernel(tc, qT, k_words, k_scales, kn, qn, offs, out):
@@ -80,15 +81,15 @@ def tile_attend_tok_dist_topk_kernel(tc, qT, k_words, k_scales, kn, qn, offs, ou
                 dst.rearrange("p (c i) t -> p c t i", i=4), src.rearrange("p t (c i) -> p c t i", i=4), COPY, scale=-2.0
             )
 
-        def quantize(h, bf):
+        def quantize(h, bf, cols):
             nc.vector.quantize_mx(
-                out=q_codes[h][:].bitcast(FP8X4),
-                scales=q_scale[h][:],
-                in_=bf[:].rearrange("p c t -> p (c t)"),
+                out=q_codes[h][:, cols].bitcast(FP8X4),
+                scales=q_scale[h][:, cols],
+                in_=bf[:, cols, :].rearrange("p c t -> p (c t)"),
             )
 
         cast(bf_early[:], q_early[:])
-        quantize(0, bf_early)
+        quantize(0, bf_early, slice(0, HALF))
 
         qn_ps = psum.tile([P, PACK, P], F32, name="qn_ps", tag="bank6")
         for j in range(PACK):
@@ -108,7 +109,9 @@ def tile_attend_tok_dist_topk_kernel(tc, qT, k_words, k_scales, kn, qn, offs, ou
 
         for pair, split in enumerate(SCALAR_COLS):
             planes = slice(2 * pair, 2 * pair + 2)
-            cast(bf_late[:, 0:split, planes], q_late[:, planes, 0:split])
+            cuts = (0, split) if pair == 0 else (0, QUARTER, split)
+            for lo, hi in zip(cuts, cuts[1:]):
+                cast(bf_late[:, lo:hi, planes], q_late[:, planes, lo:hi])
             nc.gpsimd.tensor_scalar(
                 bf_late[:, split:HALF, planes],
                 q_late[:, planes, split:HALF].rearrange("p t c -> p c t"),
@@ -118,29 +121,32 @@ def tile_attend_tok_dist_topk_kernel(tc, qT, k_words, k_scales, kn, qn, offs, ou
                 ADD,
             )
 
-        def piece(h, m, res):
+        def piece(h, m, res, bank, lo=0, hi=HALF):
             slots = slice(m * P, (m + 1) * P)
-            cols = slice(h * HALF, (h + 1) * HALF)
-            acc = psum.tile([P, HALF], F32, name="acc%d_%d" % (h, m), tag="bank%d" % (4 * h + m))
+            cols = slice(h * HALF + lo, h * HALF + hi)
+            acc = psum.tile([P, hi - lo], F32, name="acc%d_%d_%d" % (h, m, lo), tag="bank%d" % bank)
             nc.tensor.matmul_mx(
                 out=acc[:],
                 lhsT=listed[:, slots].bitcast(FP8X4),
                 lhsT_scale=k_scale[:, slots],
-                rhs=q_codes[h][:].bitcast(FP8X4),
-                rhs_scale=q_scale[h][:],
+                rhs=q_codes[h][:, lo:hi].bitcast(FP8X4),
+                rhs_scale=q_scale[h][:, lo:hi],
                 start=True,
                 stop=True,
             )
             nc.vector.scalar_tensor_tensor(res, acc[:], kn_cols[:, m : m + 1], qn_rows[:, cols], ADD, ADD)
             nc.sync.dma_start(out[0, slots, cols], res)
 
-        first = [held.tile([P, HALF], F32, name="first%d" % m, align_bytes=64) for m in range(2)]
-        for m in range(2):
-            piece(0, m, first[m][:])
-        quantize(1, bf_late)
-        second = held.tile([P, 2 * HALF], F32, name="second", tag="bf_late", align_bytes=64)
-        for m in range(2):
-            piece(0, 2 + m, second[:, m * HALF : (m + 1) * HALF])
-        for m in range(4):
+        first = [held.tile([P, HALF], F32, name="first%d" % m, align_bytes=64) for m in range(3)]
+        for m in range(3):
+            piece(0, m, first[m][:], m)
+        quantize(1, bf_late, slice(0, QUARTER))
+        quantize(1, bf_late, slice(QUARTER, HALF))
+        second = held.tile([P, HALF], F32, name="second", tag="bf_late", align_bytes=64)
+        piece(0, 3, second[:], 3)
+        for u in range(2):
+            narrow = held.tile([P, QUARTER], F32, name="narrow%d" % u, align_bytes=64)
+            piece(1, 0, narrow[:], 4 + u, u * QUARTER, (u + 1) * QUARTER)
+        for m in range(1, 4):
             last = held.tile([P, HALF], F32, name="last%d" % m, align_bytes=64)
-            piece(1, m, last[:])
+            piece(1, m, last[:], (5 + m) % 8)

@@ -103,9 +103,8 @@ def tile_attend_tok_dist_topk_kernel(tc, qT, k_words, k_scales, kn, qn, offs, ou
         nc.scalar.copy(kn_cols[:], kn_ps[:, :, KN_ROW])
 
         listed = held.tile([P, N], U32, name="listed", tag="bf_early", align_bytes=64)
-        for g in range(2):
-            part = listed[:, g * N // 2 : (g + 1) * N // 2]
-            nc.vector.tensor_copy(part, word_pool[:].indirect(offsets[:, g * N // 32 : (g + 1) * N // 32]))
+        for lo, hi in ((0, P), (P, 2 * P), (2 * P, N)):
+            nc.vector.tensor_copy(listed[:, lo:hi], word_pool[:].indirect(offsets[:, lo // 16 : hi // 16]))
 
         for pair, split in enumerate(SCALAR_COLS):
             planes = slice(2 * pair, 2 * pair + 2)
@@ -121,32 +120,32 @@ def tile_attend_tok_dist_topk_kernel(tc, qT, k_words, k_scales, kn, qn, offs, ou
                 ADD,
             )
 
-        def piece(h, m, res, bank, lo=0, hi=HALF):
+        def piece(h, m, res, cuts=(0, HALF), stores=(0, HALF)):
             slots = slice(m * P, (m + 1) * P)
-            cols = slice(h * HALF + lo, h * HALF + hi)
-            acc = psum.tile([P, hi - lo], F32, name="acc%d_%d_%d" % (h, m, lo), tag="bank%d" % bank)
-            nc.tensor.matmul_mx(
-                out=acc[:],
-                lhsT=listed[:, slots].bitcast(FP8X4),
-                lhsT_scale=k_scale[:, slots],
-                rhs=q_codes[h][:, lo:hi].bitcast(FP8X4),
-                rhs_scale=q_scale[h][:, lo:hi],
-                start=True,
-                stop=True,
-            )
+            cols = slice(h * HALF, (h + 1) * HALF)
+            acc = psum.tile([P, HALF], F32, name="acc%d_%d" % (h, m), tag="bank%d" % (4 * h + m))
+            for lo, hi in zip(cuts, cuts[1:]):
+                nc.tensor.matmul_mx(
+                    out=acc[:, lo:hi],
+                    lhsT=listed[:, slots].bitcast(FP8X4),
+                    lhsT_scale=k_scale[:, slots],
+                    rhs=q_codes[h][:, lo:hi].bitcast(FP8X4),
+                    rhs_scale=q_scale[h][:, lo:hi],
+                    start=True,
+                    stop=True,
+                )
             nc.vector.scalar_tensor_tensor(res, acc[:], kn_cols[:, m : m + 1], qn_rows[:, cols], ADD, ADD)
-            nc.sync.dma_start(out[0, slots, cols], res)
+            for lo, hi in zip(stores, stores[1:]):
+                nc.sync.dma_start(out[0, slots, h * HALF + lo : h * HALF + hi], res[:, lo:hi])
 
-        first = [held.tile([P, HALF], F32, name="first%d" % m, align_bytes=64) for m in range(3)]
-        for m in range(3):
-            piece(0, m, first[m][:], m)
+        first = [held.tile([P, HALF], F32, name="first%d" % m, align_bytes=64) for m in range(2)]
+        for m in range(2):
+            piece(0, m, first[m][:], stores=(0, 96, 176, HALF))
         quantize(1, bf_late, slice(0, QUARTER))
         quantize(1, bf_late, slice(QUARTER, HALF))
-        second = held.tile([P, HALF], F32, name="second", tag="bf_late", align_bytes=64)
-        piece(0, 3, second[:], 3)
-        for u in range(2):
-            narrow = held.tile([P, QUARTER], F32, name="narrow%d" % u, align_bytes=64)
-            piece(1, 0, narrow[:], 4 + u, u * QUARTER, (u + 1) * QUARTER)
-        for m in range(1, 4):
+        second = held.tile([P, 2 * HALF], F32, name="second", tag="bf_late", align_bytes=64)
+        for m in range(2):
+            piece(0, 2 + m, second[:, m * HALF : (m + 1) * HALF])
+        for m in range(4):
             last = held.tile([P, HALF], F32, name="last%d" % m, align_bytes=64)
-            piece(1, m, last[:], (5 + m) % 8)
+            piece(1, m, last[:], (0, QUARTER, HALF) if m == 0 else (0, HALF))

@@ -23,20 +23,21 @@ PACK = 4
 KN_ROW = P - 1
 HALF = NQ // 2
 SCALE_ROW0 = 48
-SCALAR_COLS = (176, 176)
 QUARTER = NQ // 4
+LATE_LOADS = ((0, 0, HALF, 144), (1, 0, QUARTER, QUARTER), (1, QUARTER, HALF, 200))
 
 
 def tile_attend_tok_dist_topk_kernel(tc, qT, k_words, k_scales, kn, qn, offs, out):
     nc = tc.nc
     with ExitStack() as ctx:
         held = ctx.enter_context(tc.tile_pool(name="held", bufs=1))
+        shared = ctx.enter_context(tc.tile_pool(name="shared", bufs=1))
         psum = ctx.enter_context(tc.psum_pool(name="psum", bufs=1))
 
         offsets = held.tile([P, N // 16], U16, name="offsets")
         nc.sync.dma_start(offsets[:], offs)
 
-        scale_pool = held.tile([P, T], U8, name="scale_pool", tag="scale_pool", align_bytes=64)
+        scale_pool = shared.tile([P, T], U8, name="scale_pool", offset=1536, align_bytes=64)
         kn_pool = held.tile([P, T], F32, name="kn_pool", align_bytes=64)
         word_pool = held.tile([P, T], U32, name="word_pool", align_bytes=64)
         q_early = held.tile([P, PACK, HALF], F32, name="q_early", align_bytes=64)
@@ -65,9 +66,12 @@ def tile_attend_tok_dist_topk_kernel(tc, qT, k_words, k_scales, kn, qn, offs, ou
         for g in range(4):
             rows = scale_listed[SCALE_ROW0 + 4 * g : SCALE_ROW0 + 4 * g + 4, :]
             nc.sync.dma_start(k_scale[32 * g : 32 * g + 4, :].bitcast(I32), rows.bitcast(I32))
-        q_late = held.tile([P, PACK, HALF], F32, name="q_late", tag="scale_pool", align_bytes=64)
-        nc.sync.dma_start(q_late[:, 0:2, :], q_rows[:, 0:2, HALF:NQ])
-        nc.sync.dma_start(q_late[:, 2:4, :], q_rows[:, 2:4, HALF:NQ])
+        q_late = []
+        at = 0
+        for i, (pair, lo, hi, split) in enumerate(LATE_LOADS):
+            q_late.append(shared.tile([P, 2, hi - lo], F32, name="q_late%d" % i, offset=at, align_bytes=64))
+            nc.sync.dma_start(q_late[i][:], q_rows[:, 2 * pair : 2 * pair + 2, HALF + lo : HALF + hi])
+            at = at + 8 * (hi - lo)
         kn_listed = held.tile([P, N], F32, name="kn_listed", align_bytes=64)
         nc.vector.tensor_copy(kn_listed[:], kn_pool[:].indirect(offsets[:]))
 
@@ -106,19 +110,18 @@ def tile_attend_tok_dist_topk_kernel(tc, qT, k_words, k_scales, kn, qn, offs, ou
         for lo, hi in ((0, P), (P, 2 * P), (2 * P, N)):
             nc.vector.tensor_copy(listed[:, lo:hi], word_pool[:].indirect(offsets[:, lo // 16 : hi // 16]))
 
-        for pair, split in enumerate(SCALAR_COLS):
+        for raw, (pair, lo, hi, split) in zip(q_late, LATE_LOADS):
             planes = slice(2 * pair, 2 * pair + 2)
-            cuts = (0, split) if pair == 0 else (0, QUARTER, split)
-            for lo, hi in zip(cuts, cuts[1:]):
-                cast(bf_late[:, lo:hi, planes], q_late[:, planes, lo:hi])
-            nc.gpsimd.tensor_scalar(
-                bf_late[:, split:HALF, planes],
-                q_late[:, planes, split:HALF].rearrange("p t c -> p c t"),
-                -2.0,
-                0.0,
-                MULT,
-                ADD,
-            )
+            cast(bf_late[:, lo:split, planes], raw[:, :, 0 : split - lo])
+            if split < hi:
+                nc.gpsimd.tensor_scalar(
+                    bf_late[:, split:hi, planes],
+                    raw[:, :, split - lo : hi - lo].rearrange("p t c -> p c t"),
+                    -2.0,
+                    0.0,
+                    MULT,
+                    ADD,
+                )
 
         def piece(h, m, res, cuts=(0, HALF), stores=(0, HALF)):
             slots = slice(m * P, (m + 1) * P)
@@ -140,7 +143,7 @@ def tile_attend_tok_dist_topk_kernel(tc, qT, k_words, k_scales, kn, qn, offs, ou
 
         first = [held.tile([P, HALF], F32, name="first%d" % m, align_bytes=64) for m in range(2)]
         for m in range(2):
-            piece(0, m, first[m][:], stores=(0, 96, 176, HALF))
+            piece(0, m, first[m][:], stores=(0, 96, 176, HALF) if m == 0 else (0, QUARTER, HALF))
         quantize(1, bf_late, slice(0, QUARTER))
         quantize(1, bf_late, slice(QUARTER, HALF))
         second = held.tile([P, 2 * HALF], F32, name="second", tag="bf_late", align_bytes=64)

@@ -22,7 +22,7 @@ P = 128
 PACK = 4
 KN_ROW = P - 1
 HALF = NQ // 2
-SCALE_ROW0 = 48
+SCALE_ROW0 = P - 16
 QUARTER = NQ // 4
 LATE_LOADS = ((0, 0, HALF, 144), (1, 0, QUARTER, QUARTER), (1, QUARTER, HALF, 200))
 
@@ -54,10 +54,9 @@ def tile_attend_tok_dist_topk_kernel(tc, qT, k_words, k_scales, kn, qn, offs, ou
         nc.sync.dma_start(word_pool[:].bitcast(I32), words)
 
         nc.gpsimd.memset(scale_pool[0:SCALE_ROW0, :].bitcast(I32), 0)
-        nc.gpsimd.memset(scale_pool[SCALE_ROW0 + 16 : P, :].bitcast(I32), 0)
-        nc.vector.memset(kn_pool[0:KN_ROW, 0:895], 0.0)
-        nc.vector.memset(kn_pool[0:KN_ROW, 895:1792], 0.0)
-        nc.gpsimd.memset(kn_pool[0:KN_ROW, 1792:T], 0.0)
+        nc.vector.memset(kn_pool[0:KN_ROW, 0:639], 0.0)
+        nc.vector.memset(kn_pool[0:KN_ROW, 639:1280], 0.0)
+        nc.gpsimd.memset(kn_pool[0:KN_ROW, 1280:T], 0.0)
         nc.gpsimd.memset(k_scale[:].bitcast(I32), 0)
         make_identity(nc, ident[:])
 

@@ -24,7 +24,7 @@ KN_ROW = P - 1
 HALF = NQ // 2
 SCALE_ROW0 = P - 16
 QUARTER = NQ // 4
-LATE_LOADS = ((0, 0, HALF, 144), (1, 0, QUARTER, QUARTER), (1, QUARTER, HALF, 200))
+LATE_LOADS = ((0, 0, HALF, 160), (1, 0, 160, 96), (1, 160, HALF, HALF))
 
 
 def tile_attend_tok_dist_topk_kernel(tc, qT, k_words, k_scales, kn, qn, offs, out):

@@ -122,13 +122,15 @@ def tile_attend_tok_dist_topk_kernel(tc, qT, k_words, k_scales, kn, qn, offs, ou
                     ADD,
                 )
 
-        def piece(h, m, res, cuts=(0, HALF), stores=(0, HALF)):
+        def piece(h, m, res, bank, cuts=(0, HALF), stores=None):
             slots = slice(m * P, (m + 1) * P)
-            cols = slice(h * HALF, (h + 1) * HALF)
-            acc = psum.tile([P, HALF], F32, name="acc%d_%d" % (h, m), tag="bank%d" % (4 * h + m))
+            start, end = cuts[0], cuts[-1]
+            cols = slice(h * HALF + start, h * HALF + end)
+            stores = stores or (start, end)
+            acc = psum.tile([P, end - start], F32, name="acc%d_%d_%d" % (h, m, start), tag="bank%d" % bank)
             for lo, hi in zip(cuts, cuts[1:]):
                 nc.tensor.matmul_mx(
-                    out=acc[:, lo:hi],
+                    out=acc[:, lo - start : hi - start],
                     lhsT=listed[:, slots].bitcast(FP8X4),
                     lhsT_scale=k_scale[:, slots],
                     rhs=q_codes[h][:, lo:hi].bitcast(FP8X4),
@@ -138,16 +140,17 @@ def tile_attend_tok_dist_topk_kernel(tc, qT, k_words, k_scales, kn, qn, offs, ou
                 )
             nc.vector.scalar_tensor_tensor(res, acc[:], kn_cols[:, m : m + 1], qn_rows[:, cols], ADD, ADD)
             for lo, hi in zip(stores, stores[1:]):
-                nc.sync.dma_start(out[0, slots, h * HALF + lo : h * HALF + hi], res[:, lo:hi])
+                nc.sync.dma_start(out[0, slots, h * HALF + lo : h * HALF + hi], res[:, lo - start : hi - start])
 
         first = [held.tile([P, HALF], F32, name="first%d" % m, align_bytes=64) for m in range(2)]
-        for m in range(2):
-            piece(0, m, first[m][:], stores=(0, 96, 176, HALF) if m == 0 else (0, QUARTER, HALF))
+        piece(0, 0, first[0][:, 0:QUARTER], 0, (0, QUARTER))
+        piece(0, 0, first[0][:, QUARTER:HALF], 5, (QUARTER, HALF))
+        piece(0, 1, first[1][:], 1, stores=(0, 96, 176, HALF))
         quantize(1, bf_late, slice(0, QUARTER))
         quantize(1, bf_late, slice(QUARTER, HALF))
         second = held.tile([P, 2 * HALF], F32, name="second", tag="bf_late", align_bytes=64)
         for m in range(2):
-            piece(0, 2 + m, second[:, m * HALF : (m + 1) * HALF])
+            piece(0, 2 + m, second[:, m * HALF : (m + 1) * HALF], 2 + m)
         for m in range(4):
             last = held.tile([P, HALF], F32, name="last%d" % m, align_bytes=64)
-            piece(1, m, last[:], (0, QUARTER, HALF) if m == 0 else (0, HALF))
+            piece(1, m, last[:], 4 + m, (0, QUARTER, HALF) if m == 0 else (0, HALF))

@@ -45,7 +45,7 @@ def tile_attend_tok_dist_topk_kernel(tc, qT, k_words, k_scales, kn, qn, offs, ou
         k_scale = held.tile([P, N], U8, name="k_scale", align_bytes=64)
         ident = held.tile([P, P], F32, name="ident", align_bytes=64)
 
-        nc.sync.dma_start(scale_pool[SCALE_ROW0 : SCALE_ROW0 + 16, :].bitcast(I32), k_scales[0].bitcast(I32))
+        nc.scalar.dma_start(scale_pool[SCALE_ROW0 : SCALE_ROW0 + 16, :].bitcast(I32), k_scales[0].bitcast(I32))
         q_rows = qT[0].rearrange("(p j) w -> p j w", j=PACK)
         words = k_words[0].rearrange("p t r -> p (t r)").bitcast(I32)
         nc.sync.dma_start(q_early[:], q_rows[:, :, 0:HALF])

from contextlib import ExitStack

import concourse.mybir as mybir
from concourse.masks import make_identity

T, N, D, NQ = 2048, 512, 512, 512
FLOPS = 2 * N * D * NQ

F32 = mybir.dt.float32
BF16 = mybir.dt.bfloat16
I32 = mybir.dt.int32
U32 = mybir.dt.uint32
U16 = mybir.dt.uint16
U8 = mybir.dt.uint8
FP8X4 = mybir.dt.float8_e4m3fn_x4
ADD = mybir.AluOpType.add
MULT = mybir.AluOpType.mult
COPY = mybir.ActivationFunctionType.Copy
IDENT = mybir.ActivationFunctionType.Identity

P = 128
PACK = 4
KN_ROW = P - 1
HALF = NQ // 2
SCALE_ROW0 = P - 16
QUARTER = NQ // 4
LATE_LOADS = ((0, 0, HALF, 160), (1, 0, 160, 96), (1, 160, HALF, HALF))


def tile_attend_tok_dist_topk_kernel(tc, qT, k_words, k_scales, kn, qn, offs, out):
    nc = tc.nc
    with ExitStack() as ctx:
        held = ctx.enter_context(tc.tile_pool(name="held", bufs=1))
        shared = ctx.enter_context(tc.tile_pool(name="shared", bufs=1))
        psum = ctx.enter_context(tc.psum_pool(name="psum", bufs=1))

        offsets = held.tile([P, N // 16], U16, name="offsets")
        nc.sync.dma_start(offsets[:], offs)

        scale_pool = shared.tile([P, T], U8, name="scale_pool", offset=1536, align_bytes=64)
        kn_pool = held.tile([P, T], F32, name="kn_pool", align_bytes=64)
        word_pool = held.tile([P, T], U32, name="word_pool", align_bytes=64)
        q_early = held.tile([P, PACK, HALF], F32, name="q_early", align_bytes=64)
        qn_cols = held.tile([P, PACK], F32, name="qn_cols", align_bytes=64)
        k_scale = held.tile([P, N], U8, name="k_scale", align_bytes=64)
        ident = held.tile([P, P], F32, name="ident", align_bytes=64)

        nc.scalar.dma_start(scale_pool[SCALE_ROW0 : SCALE_ROW0 + 16, :].bitcast(I32), k_scales[0].bitcast(I32))
        q_rows = qT[0].rearrange("(p j) w -> p j w", j=PACK)
        words = k_words[0].rearrange("p t r -> p (t r)").bitcast(I32)
        nc.sync.dma_start(q_early[:], q_rows[:, :, 0:HALF])
        nc.sync.dma_start(kn_pool[KN_ROW:P, :], kn[0:1, :])
        nc.sync.dma_start(qn_cols[:], qn[0, 0].rearrange("(p j) -> p j", j=PACK))
        nc.sync.dma_start(word_pool[:].bitcast(I32), words)

        nc.gpsimd.memset(scale_pool[0:SCALE_ROW0, :].bitcast(I32), 0)
        nc.vector.memset(kn_pool[0:KN_ROW, 0:639], 0.0)
        nc.vector.memset(kn_pool[0:KN_ROW, 639:1280], 0.0)
        nc.gpsimd.memset(kn_pool[0:KN_ROW, 1280:T], 0.0)
        nc.gpsimd.memset(k_scale[:].bitcast(I32), 0)
        make_identity(nc, ident[:])

        scale_listed = held.tile([P, N], U8, name="scale_listed", align_bytes=64)
        nc.vector.tensor_copy(scale_listed[:], scale_pool[:].indirect(offsets[:]))
        for g in range(4):
            rows = scale_listed[SCALE_ROW0 + 4 * g : SCALE_ROW0 + 4 * g + 4, :]
            nc.sync.dma_start(k_scale[32 * g : 32 * g + 4, :].bitcast(I32), rows.bitcast(I32))
        q_late = []
        at = 0
        for i, (pair, lo, hi, split) in enumerate(LATE_LOADS):
            q_late.append(shared.tile([P, 2, hi - lo], F32, name="q_late%d" % i, offset=at, align_bytes=64))
            nc.sync.dma_start(q_late[i][:], q_rows[:, 2 * pair : 2 * pair + 2, HALF + lo : HALF + hi])
            at = at + 8 * (hi - lo)
        kn_listed = held.tile([P, N], F32, name="kn_listed", align_bytes=64)
        nc.vector.tensor_copy(kn_listed[:], kn_pool[:].indirect(offsets[:]))

        bf_early = held.tile([P, HALF, PACK], BF16, name="bf_early", tag="bf_early", align_bytes=64)
        bf_late = held.tile([P, HALF, PACK], BF16, name="bf_late", tag="bf_late", align_bytes=64)
        q_codes = [held.tile([P, HALF], U32, name="q_codes%d" % h, align_bytes=64) for h in range(2)]
        q_scale = [held.tile([P, HALF], U8, name="q_scale%d" % h, align_bytes=64) for h in range(2)]

        def cast(dst, src):
            nc.scalar.activation(
                dst.rearrange("p (c i) t -> p c t i", i=4), src.rearrange("p t (c i) -> p c t i", i=4), COPY, scale=-2.0
            )

        def quantize(h, bf, cols):
            nc.vector.quantize_mx(
                out=q_codes[h][:, cols].bitcast(FP8X4),
                scales=q_scale[h][:, cols],
                in_=bf[:, cols, :].rearrange("p c t -> p (c t)"),
            )

        cast(bf_early[:], q_early[:])
        quantize(0, bf_early, slice(0, HALF))

        qn_ps = psum.tile([P, PACK, P], F32, name="qn_ps", tag="bank6")
        for j in range(PACK):
            nc.tensor.transpose(qn_ps[:, j, :], qn_cols[:, j : j + 1].to_broadcast([P, P]), ident[:])
        kn_ps = psum.tile([P, N // P, P], F32, name="kn_ps", tag="bank7")
        for m in range(N // P):
            nc.tensor.transpose(kn_ps[:, m, :], kn_listed[:, m * P : (m + 1) * P], ident[:])
        qn_rows = held.tile([P, NQ], F32, name="qn_rows", align_bytes=64)
        nc.scalar.copy(qn_rows[:].rearrange("p (c j) -> p c j", j=PACK), qn_ps[:].rearrange("p j c -> p c j"))
        kn_cols = held.tile([P, N // P], F32, name="kn_cols", align_bytes=64)
        nc.scalar.copy(kn_cols[:], kn_ps[:, :, KN_ROW])

        listed = held.tile([P, N], U32, name="listed", tag="bf_early", align_bytes=64)
        for lo, hi in ((0, P), (P, 2 * P), (2 * P, N)):
            nc.vector.tensor_copy(listed[:, lo:hi], word_pool[:].indirect(offsets[:, lo // 16 : hi // 16]))

        for raw, (pair, lo, hi, split) in zip(q_late, LATE_LOADS):
            planes = slice(2 * pair, 2 * pair + 2)
            cast(bf_late[:, lo:split, planes], raw[:, :, 0 : split - lo])
            if split < hi:
                nc.gpsimd.tensor_scalar(
                    bf_late[:, split:hi, planes],
                    raw[:, :, split - lo : hi - lo].rearrange("p t c -> p c t"),
                    -2.0,
                    0.0,
                    MULT,
                    ADD,
                )

        def piece(h, m, res, bank, cuts=(0, HALF), stores=None):
            slots = slice(m * P, (m + 1) * P)
            start, end = cuts[0], cuts[-1]
            cols = slice(h * HALF + start, h * HALF + end)
            stores = stores or (start, end)
            acc = psum.tile([P, end - start], F32, name="acc%d_%d_%d" % (h, m, start), tag="bank%d" % bank)
            for lo, hi in zip(cuts, cuts[1:]):
                nc.tensor.matmul_mx(
                    out=acc[:, lo - start : hi - start],
                    lhsT=listed[:, slots].bitcast(FP8X4),
                    lhsT_scale=k_scale[:, slots],
                    rhs=q_codes[h][:, lo:hi].bitcast(FP8X4),
                    rhs_scale=q_scale[h][:, lo:hi],
                    start=True,
                    stop=True,
                )
            nc.vector.scalar_tensor_tensor(res, acc[:], kn_cols[:, m : m + 1], qn_rows[:, cols], ADD, ADD)
            for lo, hi in zip(stores, stores[1:]):
                nc.sync.dma_start(out[0, slots, h * HALF + lo : h * HALF + hi], res[:, lo - start : hi - start])

        first = [held.tile([P, HALF], F32, name="first%d" % m, align_bytes=64) for m in range(2)]
        piece(0, 0, first[0][:, 0:QUARTER], 0, (0, QUARTER))
        piece(0, 0, first[0][:, QUARTER:HALF], 5, (QUARTER, HALF))
        piece(0, 1, first[1][:], 1, stores=(0, 96, 176, HALF))
        quantize(1, bf_late, slice(0, QUARTER))
        quantize(1, bf_late, slice(QUARTER, HALF))
        second = held.tile([P, 2 * HALF], F32, name="second", tag="bf_late", align_bytes=64)
        for m in range(2):
            piece(0, 2 + m, second[:, m * HALF : (m + 1) * HALF], 2 + m)
        for m in range(4):
            last = held.tile([P, HALF], F32, name="last%d" % m, align_bytes=64)
            piece(1, m, last[:], 4 + m, (0, QUARTER, HALF) if m == 0 else (0, HALF))
